import numpy as np
import ml_dtypes


def mxq(x, axis, fmt="e4m3"):
    dtype, down = {"e4m3": (ml_dtypes.float8_e4m3fn, 7), "e5m2": (ml_dtypes.float8_e5m2, 14)}[fmt]
    v = np.moveaxis(np.asarray(x, np.float32).astype(ml_dtypes.bfloat16).astype(np.float64), axis, -1)
    blocks = v.reshape(v.shape[:-1] + (-1, 32))
    amax = np.abs(blocks).max(-1, keepdims=True)
    byte = np.maximum(np.where(amax > 0, np.frexp(amax)[1] - 1 + 127, 0) - down, 1)
    scale = np.exp2(byte - 127.0)
    codes = (blocks / scale).astype(np.float32).astype(dtype).astype(np.float64)
    return np.moveaxis((codes * scale).reshape(v.shape), -1, axis)


WIDE = False


def mx_kscale(k):
    if not WIDE:
        return np.ones(k)
    levels = np.array([10, -10, 5, -5, 0])
    if k % 512:
        return np.exp2(np.random.permutation(np.resize(levels, k // 32))).repeat(32)
    a = np.empty((k // 512, 16))
    for p in range(k // 512):
        a[p, :8] = np.random.permutation(np.resize(levels, 8))
        for g in range(8):
            far = levels[np.abs(levels - a[p, g]) >= 10]
            a[p, g + 8] = far[np.random.randint(len(far))]
    return np.exp2(a.ravel()).repeat(32)


def f64(x):
    return np.asarray(x).astype(np.float64)


def striped(idx):
    return np.tile(idx.reshape(-1, 16).T, (8, 1)).astype(np.uint16)


def unstriped(offs):
    return offs[:16].T.reshape(-1).astype(np.int64)


def pack_weight(w):
    k, n = w.shape
    w = f64(np.asarray(w, np.float32).astype(ml_dtypes.bfloat16)).reshape(k // 32, 32, n)
    amax = np.abs(w).max(1)
    byte = np.clip(np.where(amax > 0, np.frexp(amax)[1] - 1 + 127 - 7, 1), 1, 254)
    scaled = (w * np.exp2(127.0 - byte)[:, None, :]).reshape(k, n).astype(np.float32)
    words = np.ascontiguousarray(scaled.reshape(k // 512, 128, 4, n).transpose(0, 1, 3, 2)).astype(ml_dtypes.float8_e4m3fn).view(np.uint8)
    return words, np.ascontiguousarray(byte.astype(np.uint8).reshape(k // 512, 16, n))


def unpack_weight(words, scales):
    g, p, n, _ = words.shape
    vals = np.ascontiguousarray(words).view(ml_dtypes.float8_e4m3fn).astype(np.float64) * np.repeat(np.exp2(scales.astype(np.float64) - 127.0), 8, axis=1)[..., None]
    return vals.transpose(0, 1, 3, 2).reshape(g * 512, n)

def planes(y):
    n, m = y.shape
    v = y.astype(np.float32).astype(ml_dtypes.bfloat16).astype(np.float64).reshape(n // 32, 32, m)
    top = np.abs(v).max(1)
    byte = np.clip(np.where(top > 0, np.frexp(top)[1] - 1 + 127 - 7, 1), 1, 254)
    codes = (v * np.exp2(127.0 - byte)[:, None, :]).reshape(n, m).astype(np.float32).astype(ml_dtypes.float8_e4m3fn).view(np.uint8)
    words = codes.reshape(n // 512, 128, 4, m).transpose(0, 1, 3, 2)
    return np.ascontiguousarray(words), np.ascontiguousarray(byte.astype(np.uint8).reshape(n // 512, 16, m))


K, T, N, U = 512, 512, 512, 1024


def setup_inputs():
    n = np.random.standard_normal
    s = mx_kscale(K)[:, None]
    packed_xT = pack_weight(n((K, T)) * s)
    return {
        "x_words": packed_xT[0],
        "x_scales": packed_xT[1],
        "mem": n((N, U)).astype(np.float32),
        "w1": (n((K, N)) / np.sqrt(K) / s).astype(np.float32),
        "slot": striped(np.random.permutation(U)[:T]),
    }


def reference(x_words, x_scales, mem, w1, slot):
    xq = unpack_weight(x_words, x_scales)
    y = np.tanh(mxq(f64(w1), 0, "e4m3").T @ xq)
    out = f64(mem).copy()
    out[:, unstriped(slot)] = y
    return (out,) + planes(out)

@@ -1,0 +1,126 @@
+from contextlib import ExitStack
+
+import concourse.mybir as mybir
+
+K, T, N, U = 512, 512, 512, 1024
+FLOPS = 2 * K * T * N
+
+F32 = mybir.dt.float32
+BF16 = mybir.dt.bfloat16
+I32 = mybir.dt.int32
+U32 = mybir.dt.uint32
+U16 = mybir.dt.uint16
+U8 = mybir.dt.uint8
+FP8X4 = mybir.dt.float8_e4m3fn_x4
+TANH = mybir.ActivationFunctionType.Tanh
+
+P = 128
+PACK = 4
+QUADS = 4
+
+
+def tile_picked_wkvput_tanh_lo_kernel(tc, x_words, x_scales, mem, w1, slot, out_0, out_1, out_2):
+    nc = tc.nc
+    with ExitStack() as ctx:
+        sb = ctx.enter_context(tc.tile_pool(name="sb", bufs=1))
+        ps = ctx.enter_context(tc.psum_pool(name="ps", bufs=1))
+
+        offsets = sb.tile([P, T // 16], U16, name="offsets")
+        x_codes = sb.tile([P, T], U32, name="x_codes", align_bytes=64)
+        x_plane = sb.tile([P, T], U8, name="x_plane", align_bytes=64)
+        warm_in = sb.tile([P, 8], F32, name="warm_in")
+        warm_out = sb.tile([P, 8], F32, name="warm_out")
+
+        nc.vector.memset(x_plane[:].bitcast(I32), 0)
+        nc.vector.memset(warm_in[:], 0.0)
+        for q in range(QUADS):
+            nc.scalar.dma_start(out=x_plane[32 * q : 32 * q + 4, :].bitcast(I32), in_=x_scales[0, 4 * q : 4 * q + 4, :].bitcast(I32))
+        nc.scalar.activation(warm_out[:, 0:1], warm_in[:, 0:1], TANH)
+
+        HALF = N // 2
+        MH = HALF // PACK
+        w_rows = w1.rearrange("(p j) n -> p j n", j=PACK)
+        w_raw = []
+        for h in range(2):
+            raw = sb.tile([P, PACK, HALF], F32, name=f"w_raw{h}")
+            nc.sync.dma_start(out=raw[:], in_=w_rows[:, :, h * HALF : (h + 1) * HALF])
+            w_raw.append(raw)
+        nc.sync.dma_start(out=x_codes[:].bitcast(I32), in_=x_words[0].rearrange("p n t -> p (n t)").bitcast(I32))
+        nc.sync.dma_start(offsets[:], slot)
+        mem_rows = mem.rearrange("(p t) u -> p t u", t=PACK)
+        out_rows = out_0.rearrange("(p t) u -> p t u", t=PACK)
+        window = []
+        for t in range(PACK):
+            win = sb.tile([P, U], F32, name=f"window{t}")
+            nc.sync.dma_start(out=win[:], in_=mem_rows[:, t, :])
+            window.append(win)
+
+        w_codes = [sb.tile([P, P], U32, name=f"w_codes{t}", align_bytes=64) for t in range(PACK)]
+        w_plane = [sb.tile([P, P], U8, name=f"w_plane{t}", align_bytes=64) for t in range(PACK)]
+        for h in range(2):
+            dealt = sb.tile([P, PACK, MH, PACK], BF16, name=f"w_dealt{h}", align_bytes=64)
+            nc.vector.tensor_copy(
+                out=dealt[:].rearrange("p t m j -> p m j t"),
+                in_=w_raw[h][:].rearrange("p j (m t) -> p m j t", t=PACK),
+            )
+            for t in range(PACK):
+                nc.vector.quantize_mx(
+                    out=w_codes[t][:, h * MH : (h + 1) * MH].bitcast(FP8X4),
+                    scales=w_plane[t][:, h * MH : (h + 1) * MH],
+                    in_=dealt[:, t].rearrange("p m j -> p (m j)"),
+                )
+
+        def project(t, y, y0, c0, c1):
+            acc = ps.tile([P, c1 - c0], F32, name=f"acc{t}_{c0}")
+            nc.tensor.matmul_mx(
+                out=acc[:],
+                lhsT=w_codes[t][:].bitcast(FP8X4),
+                lhsT_scale=w_plane[t][:],
+                rhs=x_codes[:, c0:c1].bitcast(FP8X4),
+                rhs_scale=x_plane[:, c0:c1],
+                start=True,
+                stop=True,
+            )
+            nc.scalar.activation(y[:, c0 - y0 : c1 - y0], acc[:], TANH)
+
+        pieces = [[(0, 128, [(0, 128)]), (128, 512, [(128, 256), (256, 512)])]] + [[(0, 512, [(0, 512)])]] * 3
+        values = []
+        for t in range(PACK):
+            for a, b, parts in pieces[t]:
+                y = sb.tile([P, b - a], F32, name=f"y{t}_{a}")
+                for c0, c1 in parts:
+                    project(t, y, a, c0, c1)
+                values.append((t, a, b, y))
+
+        chunks = [(0, 512), (512, 768), (768, 1024)]
+        grouped = sb.tile([P, U, PACK], BF16, name="grouped", align_bytes=64)
+        o_codes = [sb.tile([P, b - a], U32, name=f"o_codes{a}", align_bytes=64) for a, b in chunks]
+        o_plane = sb.tile([P, U], U8, name="o_plane", align_bytes=64)
+
+        for t, a, b, y in values:
+            nc.vector.tensor_copy(window[t][:].indirect(offsets[:, a // 16 : b // 16]), y[:])
+            if b == T:
+                nc.sync.dma_start(out=out_rows[:, t, :], in_=window[t][:])
+                if t < 2:
+                    nc.scalar.copy(out=grouped[:, :, t], in_=window[t][:])
+                elif t == 2:
+                    nc.scalar.copy(out=grouped[:, 0:512, 2:4], in_=window[t][:, 0:512].unsqueeze(2).to_broadcast([P, 512, 2]))
+                    nc.scalar.copy(out=grouped[:, 512:U, t], in_=window[t][:, 512:U])
+                else:
+                    for g, (c0, c1) in enumerate(chunks):
+                        if g == 0:
+                            nc.vector.tensor_copy(out=grouped[:, c0:c1, t], in_=window[t][:, c0:c1])
+                        else:
+                            nc.scalar.copy(out=grouped[:, c0:c1, t], in_=window[t][:, c0:c1])
+
+        words_out = out_1[0].rearrange("p n t -> p (n t)").bitcast(I32)
+        for g, (c0, c1) in enumerate(chunks):
+            nc.vector.quantize_mx(
+                out=o_codes[g][:].bitcast(FP8X4),
+                scales=o_plane[:, c0:c1],
+                in_=grouped[:, c0:c1, :].rearrange("p c t -> p (c t)"),
+            )
+            nc.sync.dma_start(out=words_out[:, c0:c1], in_=o_codes[g][:].bitcast(I32))
+        for q in range(QUADS):
+            queue = nc.scalar if q % 2 == 0 else nc.sync
+            queue.dma_start(out=out_2[0, 4 * q : 4 * q + 4, :].bitcast(I32), in_=o_plane[32 * q : 32 * q + 4, :].bitcast(I32))

@@ -17,6 +17,7 @@ TANH = mybir.ActivationFunctionType.Tanh
 P = 128
 PACK = 4
 QUADS = 4
+SPLIT = 560
 
 
 def tile_picked_wkvput_tanh_lo_kernel(tc, x_words, x_scales, mem, w1, slot, out_0, out_1, out_2):
@@ -28,14 +29,9 @@ def tile_picked_wkvput_tanh_lo_kernel(tc, x_words, x_scales, mem, w1, slot, out_
         offsets = sb.tile([P, T // 16], U16, name="offsets")
         x_codes = sb.tile([P, T], U32, name="x_codes", align_bytes=64)
         x_plane = sb.tile([P, T], U8, name="x_plane", align_bytes=64)
-        warm_in = sb.tile([P, 8], F32, name="warm_in")
-        warm_out = sb.tile([P, 8], F32, name="warm_out")
 
-        nc.vector.memset(x_plane[:].bitcast(I32), 0)
-        nc.vector.memset(warm_in[:], 0.0)
         for q in range(QUADS):
             nc.scalar.dma_start(out=x_plane[32 * q : 32 * q + 4, :].bitcast(I32), in_=x_scales[0, 4 * q : 4 * q + 4, :].bitcast(I32))
-        nc.scalar.activation(warm_out[:, 0:1], warm_in[:, 0:1], TANH)
 
         HALF = N // 2
         MH = HALF // PACK
@@ -57,18 +53,31 @@ def tile_picked_wkvput_tanh_lo_kernel(tc, x_words, x_scales, mem, w1, slot, out_
 
         w_codes = [sb.tile([P, P], U32, name=f"w_codes{t}", align_bytes=64) for t in range(PACK)]
         w_plane = [sb.tile([P, P], U8, name=f"w_plane{t}", align_bytes=64) for t in range(PACK)]
-        for h in range(2):
-            dealt = sb.tile([P, PACK, MH, PACK], BF16, name=f"w_dealt{h}", align_bytes=64)
+        dealt = [sb.tile([P, PACK, MH, PACK], BF16, name=f"w_dealt{h}", align_bytes=64) for h in range(2)]
+
+        def deal(h, t0, t1):
             nc.vector.tensor_copy(
-                out=dealt[:].rearrange("p t m j -> p m j t"),
-                in_=w_raw[h][:].rearrange("p j (m t) -> p m j t", t=PACK),
+                out=dealt[h][:, t0:t1].rearrange("p t m j -> p m j t"),
+                in_=w_raw[h][:].rearrange("p j (m t) -> p m j t", t=PACK)[:, :, :, t0:t1],
             )
-            for t in range(PACK):
-                nc.vector.quantize_mx(
-                    out=w_codes[t][:, h * MH : (h + 1) * MH].bitcast(FP8X4),
-                    scales=w_plane[t][:, h * MH : (h + 1) * MH],
-                    in_=dealt[:, t].rearrange("p m j -> p (m j)"),
-                )
+
+        def quantize_w(h, t):
+            nc.vector.quantize_mx(
+                out=w_codes[t][:, h * MH : (h + 1) * MH].bitcast(FP8X4),
+                scales=w_plane[t][:, h * MH : (h + 1) * MH],
+                in_=dealt[h][:, t].rearrange("p m j -> p (m j)"),
+            )
+
+        deal(0, 0, PACK)
+        quantize_w(0, 0)
+        deal(1, 0, 1)
+        quantize_w(0, 1)
+        quantize_w(0, 2)
+        quantize_w(1, 0)
+        deal(1, 1, PACK)
+        quantize_w(0, 3)
+        for t in range(1, PACK):
+            quantize_w(1, t)
 
         def project(t, y, y0, c0, c1):
             acc = ps.tile([P, c1 - c0], F32, name=f"acc{t}_{c0}")
@@ -104,22 +113,22 @@ def tile_picked_wkvput_tanh_lo_kernel(tc, x_words, x_scales, mem, w1, slot, out_
                 if t < 2:
                     nc.scalar.copy(out=grouped[:, :, t], in_=window[t][:])
                 elif t == 2:
-                    nc.scalar.copy(out=grouped[:, 0:512, 2:4], in_=window[t][:, 0:512].unsqueeze(2).to_broadcast([P, 512, 2]))
-                    nc.scalar.copy(out=grouped[:, 512:U, t], in_=window[t][:, 512:U])
+                    nc.scalar.copy(out=grouped[:, 0:SPLIT, 2:4], in_=window[t][:, 0:SPLIT].unsqueeze(2).to_broadcast([P, SPLIT, 2]))
+                    nc.scalar.copy(out=grouped[:, SPLIT:U, t], in_=window[t][:, SPLIT:U])
                 else:
-                    for g, (c0, c1) in enumerate(chunks):
-                        if g == 0:
-                            nc.vector.tensor_copy(out=grouped[:, c0:c1, t], in_=window[t][:, c0:c1])
-                        else:
-                            nc.scalar.copy(out=grouped[:, c0:c1, t], in_=window[t][:, c0:c1])
+                    for c0, c1 in ((0, 256), (256, SPLIT)):
+                        nc.vector.tensor_copy(out=grouped[:, c0:c1, t], in_=window[t][:, c0:c1])
+                    for c0, c1 in ((SPLIT, 768), (768, U)):
+                        nc.scalar.copy(out=grouped[:, c0:c1, t], in_=window[t][:, c0:c1])
 
         words_out = out_1[0].rearrange("p n t -> p (n t)").bitcast(I32)
         for g, (c0, c1) in enumerate(chunks):
-            nc.vector.quantize_mx(
-                out=o_codes[g][:].bitcast(FP8X4),
-                scales=o_plane[:, c0:c1],
-                in_=grouped[:, c0:c1, :].rearrange("p c t -> p (c t)"),
-            )
+            for c in range(c0, c1, 256):
+                nc.vector.quantize_mx(
+                    out=o_codes[g][:, c - c0 : c - c0 + 256].bitcast(FP8X4),
+                    scales=o_plane[:, c : c + 256],
+                    in_=grouped[:, c : c + 256, :].rearrange("p c t -> p (c t)"),
+                )
             nc.sync.dma_start(out=words_out[:, c0:c1], in_=o_codes[g][:].bitcast(I32))
         for q in range(QUADS):
             queue = nc.scalar if q % 2 == 0 else nc.sync

@@ -1,6 +1,7 @@
 from contextlib import ExitStack
 
 import concourse.mybir as mybir
+from concourse.masks import make_identity
 
 K, T, N, U = 512, 512, 512, 1024
 FLOPS = 2 * K * T * N
@@ -13,11 +14,18 @@ U16 = mybir.dt.uint16
 U8 = mybir.dt.uint8
 FP8X4 = mybir.dt.float8_e4m3fn_x4
 TANH = mybir.ActivationFunctionType.Tanh
+MULT = mybir.AluOpType.mult
+ADD = mybir.AluOpType.add
 
 P = 128
 PACK = 4
 QUADS = 4
+HALF = N // 2
+LH = HALF // PACK
+BANK = 512
 SPLIT = 560
+POOL_COLS = 384
+X_FIRST = 256
 
 
 def tile_picked_wkvput_tanh_lo_kernel(tc, x_words, x_scales, mem, w1, slot, out_0, out_1, out_2):
@@ -30,96 +38,137 @@ def tile_picked_wkvput_tanh_lo_kernel(tc, x_words, x_scales, mem, w1, slot, out_
         x_codes = sb.tile([P, T], U32, name="x_codes", align_bytes=64)
         x_plane = sb.tile([P, T], U8, name="x_plane", align_bytes=64)
 
-        for q in range(QUADS):
-            nc.scalar.dma_start(out=x_plane[32 * q : 32 * q + 4, :].bitcast(I32), in_=x_scales[0, 4 * q : 4 * q + 4, :].bitcast(I32))
+        def rows_of(dram, w):
+            if w < 2:
+                return dram.rearrange("(h l t) u -> h l t u", h=2, t=PACK)[w, :, 0:2, :]
+            return dram.rearrange("(p t) u -> p t u", t=PACK)[:, w, :]
 
-        HALF = N // 2
-        MH = HALF // PACK
         w_rows = w1.rearrange("(p j) n -> p j n", j=PACK)
-        w_raw = []
-        for h in range(2):
-            raw = sb.tile([P, PACK, HALF], F32, name=f"w_raw{h}")
-            nc.sync.dma_start(out=raw[:], in_=w_rows[:, :, h * HALF : (h + 1) * HALF])
-            w_raw.append(raw)
-        nc.sync.dma_start(out=x_codes[:].bitcast(I32), in_=x_words[0].rearrange("p n t -> p (n t)").bitcast(I32))
+        x_rows = x_words[0].rearrange("p n t -> p (n t)").bitcast(I32)
+        w_raw = [sb.tile([P, PACK, HALF], F32, name=f"w_raw{h}") for h in range(2)]
+        window = [sb.tile([P, U], F32, name=f"window{w}") for w in range(PACK)]
         nc.sync.dma_start(offsets[:], slot)
-        mem_rows = mem.rearrange("(p t) u -> p t u", t=PACK)
-        out_rows = out_0.rearrange("(p t) u -> p t u", t=PACK)
-        window = []
-        for t in range(PACK):
-            win = sb.tile([P, U], F32, name=f"window{t}")
-            nc.sync.dma_start(out=win[:], in_=mem_rows[:, t, :])
-            window.append(win)
+        nc.sync.dma_start(out=w_raw[0][:], in_=w_rows[:, :, 0:HALF])
+        for q in range(QUADS):
+            nc.sync.dma_start(out=x_plane[32 * q : 32 * q + 4, :].bitcast(I32), in_=x_scales[0, 4 * q : 4 * q + 4, :].bitcast(I32))
+        nc.sync.dma_start(out=x_codes[:, 0:X_FIRST].bitcast(I32), in_=x_rows[:, 0:X_FIRST])
+        nc.sync.dma_start(out=window[0][:], in_=rows_of(mem, 0))
+        nc.sync.dma_start(out=w_raw[1][:], in_=w_rows[:, :, HALF:N])
+        nc.sync.dma_start(out=x_codes[:, X_FIRST:T].bitcast(I32), in_=x_rows[:, X_FIRST:T])
+        for w in range(1, PACK):
+            nc.sync.dma_start(out=window[w][:], in_=rows_of(mem, w))
 
-        w_codes = [sb.tile([P, P], U32, name=f"w_codes{t}", align_bytes=64) for t in range(PACK)]
-        w_plane = [sb.tile([P, P], U8, name=f"w_plane{t}", align_bytes=64) for t in range(PACK)]
-        dealt = [sb.tile([P, PACK, MH, PACK], BF16, name=f"w_dealt{h}", align_bytes=64) for h in range(2)]
+        identity = sb.tile([P, P], F32, name="identity")
+        make_identity(nc, identity[:])
 
-        def deal(h, t0, t1):
-            nc.vector.tensor_copy(
-                out=dealt[h][:, t0:t1].rearrange("p t m j -> p m j t"),
-                in_=w_raw[h][:].rearrange("p j (m t) -> p m j t", t=PACK)[:, :, :, t0:t1],
-            )
+        pair_codes = [sb.tile([P, P], U32, name=f"pair_codes{h}", align_bytes=64) for h in range(2)]
+        pair_plane = [sb.tile([P, P], U8, name=f"pair_plane{h}", align_bytes=64) for h in range(2)]
+        rest_codes = sb.tile([P, 2 * P], U32, name="rest_codes", align_bytes=64)
+        rest_plane = sb.tile([P, 2 * P], U8, name="rest_plane", align_bytes=64)
 
-        def quantize_w(h, t):
+        def w_cols(h, t0):
+            return w_raw[h][:].rearrange("p j (l t) -> p l j t", t=PACK)[:, :, :, t0 : t0 + 2]
+
+        def quantize_pair(copy, h):
+            dealt = sb.tile([P, LH, 2, PACK], BF16, name=f"pair_dealt{h}", tag=f"dealt{h}", align_bytes=64)
+            copy(out=dealt[:].rearrange("p l t j -> p l j t"), in_=w_cols(h, 0))
             nc.vector.quantize_mx(
-                out=w_codes[t][:, h * MH : (h + 1) * MH].bitcast(FP8X4),
-                scales=w_plane[t][:, h * MH : (h + 1) * MH],
-                in_=dealt[h][:, t].rearrange("p m j -> p (m j)"),
+                out=pair_codes[h][:].bitcast(FP8X4),
+                scales=pair_plane[h][:],
+                in_=dealt[:].rearrange("p l t j -> p (l t j)"),
             )
 
-        deal(0, 0, PACK)
-        quantize_w(0, 0)
-        deal(1, 0, 1)
-        quantize_w(0, 1)
-        quantize_w(0, 2)
-        quantize_w(1, 0)
-        deal(1, 1, PACK)
-        quantize_w(0, 3)
-        for t in range(1, PACK):
-            quantize_w(1, t)
+        def quantize_rest(h, tag):
+            dealt = sb.tile([P, 2, LH, PACK], BF16, name=f"rest_dealt{h}", tag=tag, align_bytes=64)
+            nc.scalar.copy(out=dealt[:].rearrange("p t l j -> p l j t"), in_=w_cols(h, 2))
+            for t in range(2):
+                cols = slice(t * P + h * LH, t * P + (h + 1) * LH)
+                nc.vector.quantize_mx(
+                    out=rest_codes[:, cols].bitcast(FP8X4),
+                    scales=rest_plane[:, cols],
+                    in_=dealt[:, t].rearrange("p l j -> p (l j)"),
+                )
 
-        def project(t, y, y0, c0, c1):
-            acc = ps.tile([P, c1 - c0], F32, name=f"acc{t}_{c0}")
+        def weights(w):
+            if w < 2:
+                return pair_codes[w][:], pair_plane[w][:]
+            cols = slice((w - 2) * P, (w - 1) * P)
+            return rest_codes[:, cols], rest_plane[:, cols]
+
+        def project(w, a, b, bank):
+            codes, plane = weights(w)
+            acc = ps.tile([P, b - a], F32, name=f"acc{w}_{a}", tag=bank)
             nc.tensor.matmul_mx(
                 out=acc[:],
-                lhsT=w_codes[t][:].bitcast(FP8X4),
-                lhsT_scale=w_plane[t][:],
-                rhs=x_codes[:, c0:c1].bitcast(FP8X4),
-                rhs_scale=x_plane[:, c0:c1],
+                lhsT=codes.bitcast(FP8X4),
+                lhsT_scale=plane,
+                rhs=x_codes[:, a:b].bitcast(FP8X4),
+                rhs_scale=x_plane[:, a:b],
                 start=True,
                 stop=True,
             )
-            nc.scalar.activation(y[:, c0 - y0 : c1 - y0], acc[:], TANH)
+            y = sb.tile([P, b - a], F32, name=f"y{w}_{a}")
+            nc.scalar.activation(y[:], acc[:], TANH)
+            return (a, b, y)
 
-        pieces = [[(0, 128, [(0, 128)]), (128, 512, [(128, 256), (256, 512)])]] + [[(0, 512, [(0, 512)])]] * 3
-        values = []
-        for t in range(PACK):
-            for a, b, parts in pieces[t]:
-                y = sb.tile([P, b - a], F32, name=f"y{t}_{a}")
-                for c0, c1 in parts:
-                    project(t, y, a, c0, c1)
-                values.append((t, a, b, y))
+        quantize_pair(nc.vector.tensor_copy, 0)
+        quantize_rest(0, "rest0")
+        first = [project(0, 0, 128, "a0"), project(0, 128, X_FIRST, "a1")]
+        quantize_pair(nc.scalar.copy, 1)
+        first.append(project(0, X_FIRST, T, "a2"))
+        quantize_rest(1, "dealt1")
+        values = [first] + [[project(w, 0, T, f"b{w}")] for w in range(1, PACK)]
 
         chunks = [(0, 512), (512, 768), (768, 1024)]
         grouped = sb.tile([P, U, PACK], BF16, name="grouped", align_bytes=64)
         o_codes = [sb.tile([P, b - a], U32, name=f"o_codes{a}", align_bytes=64) for a, b in chunks]
         o_plane = sb.tile([P, U], U8, name="o_plane", align_bytes=64)
+        turned = [sb.tile([P, 4, 2, P], BF16, name=f"turned{g}") for g in range(2)]
 
-        for t, a, b, y in values:
-            nc.vector.tensor_copy(window[t][:].indirect(offsets[:, a // 16 : b // 16]), y[:])
-            if b == T:
-                nc.sync.dma_start(out=out_rows[:, t, :], in_=window[t][:])
-                if t < 2:
-                    nc.scalar.copy(out=grouped[:, :, t], in_=window[t][:])
-                elif t == 2:
-                    nc.scalar.copy(out=grouped[:, 0:SPLIT, 2:4], in_=window[t][:, 0:SPLIT].unsqueeze(2).to_broadcast([P, SPLIT, 2]))
-                    nc.scalar.copy(out=grouped[:, SPLIT:U, t], in_=window[t][:, SPLIT:U])
-                else:
-                    for c0, c1 in ((0, 256), (256, SPLIT)):
-                        nc.vector.tensor_copy(out=grouped[:, c0:c1, t], in_=window[t][:, c0:c1])
-                    for c0, c1 in ((SPLIT, 768), (768, U)):
-                        nc.scalar.copy(out=grouped[:, c0:c1, t], in_=window[t][:, c0:c1])
+        def scatter(w):
+            for a, b, y in values[w]:
+                nc.vector.tensor_copy(window[w][:].indirect(offsets[:, a // 16 : b // 16]), y[:])
+            nc.sync.dma_start(out=rows_of(out_0, w), in_=window[w][:])
+
+        for w in range(2):
+            scatter(w)
+            for g in range(2):
+                bank = ps.tile([P, 4, P], F32, name=f"there{w}_{g}", tag=f"a{g}")
+                for i in range(4):
+                    c = g * BANK + i * P
+                    nc.tensor.transpose(bank[:, i, :], window[w][:, c : c + P], identity[:])
+                nc.scalar.copy(out=turned[g][:, :, w, :], in_=bank[:])
+        for g in range(2):
+            words = turned[g][:].rearrange("p i w q -> p i (w q)").bitcast(F32)
+            bank = ps.tile([P, 4, P], F32, name=f"back{g}", tag=f"c{g}")
+            for i in range(4):
+                nc.tensor.transpose(bank[:, i, :], words[:, i, :], identity[:])
+            nc.scalar.copy(
+                out=grouped[:, g * BANK : (g + 1) * BANK, :].bitcast(F32),
+                in_=bank[:].rearrange("p i c -> p (i c)").unsqueeze(2).to_broadcast([P, BANK, 2]),
+            )
+
+        scatter(2)
+        for c0, c1 in ((0, 256), (256, POOL_COLS)):
+            nc.gpsimd.tensor_scalar(
+                out=grouped[:, c0:c1, 2:4],
+                in0=window[2][:, c0:c1].unsqueeze(2).to_broadcast([P, c1 - c0, 2]),
+                scalar1=1.0,
+                scalar2=0.0,
+                op0=MULT,
+                op1=ADD,
+            )
+        nc.scalar.copy(
+            out=grouped[:, POOL_COLS:SPLIT, 2:4],
+            in_=window[2][:, POOL_COLS:SPLIT].unsqueeze(2).to_broadcast([P, SPLIT - POOL_COLS, 2]),
+        )
+        nc.scalar.copy(out=grouped[:, SPLIT:U, 2], in_=window[2][:, SPLIT:U])
+
+        scatter(3)
+        for c0, c1 in ((0, 256), (256, SPLIT)):
+            nc.vector.tensor_copy(out=grouped[:, c0:c1, 3], in_=window[3][:, c0:c1])
+        for c0, c1 in ((SPLIT, 768), (768, U)):
+            nc.scalar.copy(out=grouped[:, c0:c1, 3], in_=window[3][:, c0:c1])
 
         words_out = out_1[0].rearrange("p n t -> p (n t)").bitcast(I32)
         for g, (c0, c1) in enumerate(chunks):

@@ -23,8 +23,7 @@ QUADS = 4
 HALF = N // 2
 LH = HALF // PACK
 BANK = 512
-SPLIT = 560
-POOL_COLS = 384
+SPLIT = 448
 X_FIRST = 256
 
 
@@ -69,18 +68,28 @@ def tile_picked_wkvput_tanh_lo_kernel(tc, x_words, x_scales, mem, w1, slot, out_
         def w_cols(h, t0):
             return w_raw[h][:].rearrange("p j (l t) -> p l j t", t=PACK)[:, :, :, t0 : t0 + 2]
 
-        def quantize_pair(copy, h):
-            dealt = sb.tile([P, LH, 2, PACK], BF16, name=f"pair_dealt{h}", tag=f"dealt{h}", align_bytes=64)
-            copy(out=dealt[:].rearrange("p l t j -> p l j t"), in_=w_cols(h, 0))
-            nc.vector.quantize_mx(
-                out=pair_codes[h][:].bitcast(FP8X4),
-                scales=pair_plane[h][:],
-                in_=dealt[:].rearrange("p l t j -> p (l t j)"),
-            )
+        def quantize_pair(copy, h, parts):
+            n = LH // parts
+            dealt = [sb.tile([P, n, 2, PACK], BF16, name=f"pair_dealt{h}_{i}", align_bytes=64) for i in range(parts)]
+            for i in range(parts):
+                copy(out=dealt[i][:].rearrange("p l t j -> p l j t"), in_=w_cols(h, 0)[:, i * n : (i + 1) * n])
+            for i in range(parts):
+                cols = slice(2 * i * n, 2 * (i + 1) * n)
+                nc.vector.quantize_mx(
+                    out=pair_codes[h][:, cols].bitcast(FP8X4),
+                    scales=pair_plane[h][:, cols],
+                    in_=dealt[i][:].rearrange("p l t j -> p (l t j)"),
+                )
 
-        def quantize_rest(h, tag):
-            dealt = sb.tile([P, 2, LH, PACK], BF16, name=f"rest_dealt{h}", tag=tag, align_bytes=64)
-            nc.scalar.copy(out=dealt[:].rearrange("p t l j -> p l j t"), in_=w_cols(h, 2))
+        def pool_round(out, in_):
+            nc.gpsimd.tensor_scalar(out=out, in0=in_, scalar1=1.0, scalar2=0.0, op0=MULT, op1=ADD)
+
+        def quantize_rest(copy, h):
+            dealt = sb.tile([P, 2, LH, PACK], BF16, name=f"rest_dealt{h}", align_bytes=64)
+            if h == 0:
+                copy(out=dealt[:].rearrange("p t l j -> p l j t"), in_=w_cols(h, 2))
+            else:
+                copy(out=dealt[:], in_=w_cols(h, 2).rearrange("p l j t -> p t l j"))
             for t in range(2):
                 cols = slice(t * P + h * LH, t * P + (h + 1) * LH)
                 nc.vector.quantize_mx(
@@ -95,31 +104,34 @@ def tile_picked_wkvput_tanh_lo_kernel(tc, x_words, x_scales, mem, w1, slot, out_
             cols = slice((w - 2) * P, (w - 1) * P)
             return rest_codes[:, cols], rest_plane[:, cols]
 
-        def project(w, a, b, bank):
+        def project(w, a, parts):
             codes, plane = weights(w)
-            acc = ps.tile([P, b - a], F32, name=f"acc{w}_{a}", tag=bank)
-            nc.tensor.matmul_mx(
-                out=acc[:],
-                lhsT=codes.bitcast(FP8X4),
-                lhsT_scale=plane,
-                rhs=x_codes[:, a:b].bitcast(FP8X4),
-                rhs_scale=x_plane[:, a:b],
-                start=True,
-                stop=True,
-            )
-            y = sb.tile([P, b - a], F32, name=f"y{w}_{a}")
-            nc.scalar.activation(y[:], acc[:], TANH)
-            return (a, b, y)
+            y = sb.tile([P, sum(n for n, bank in parts)], F32, name=f"y{w}_{a}")
+            c = a
+            for n, bank in parts:
+                acc = ps.tile([P, n], F32, name=f"acc{w}_{c}", tag=bank)
+                nc.tensor.matmul_mx(
+                    out=acc[:],
+                    lhsT=codes.bitcast(FP8X4),
+                    lhsT_scale=plane,
+                    rhs=x_codes[:, c : c + n].bitcast(FP8X4),
+                    rhs_scale=x_plane[:, c : c + n],
+                    start=True,
+                    stop=True,
+                )
+                nc.scalar.activation(y[:, c - a : c - a + n], acc[:], TANH)
+                c = c + n
+            return (a, c, y)
 
-        quantize_pair(nc.vector.tensor_copy, 0)
-        quantize_rest(0, "rest0")
-        first = [project(0, 0, 128, "a0"), project(0, 128, X_FIRST, "a1")]
-        quantize_pair(nc.scalar.copy, 1)
-        first.append(project(0, X_FIRST, T, "a2"))
-        quantize_rest(1, "dealt1")
-        values = [first] + [[project(w, 0, T, f"b{w}")] for w in range(1, PACK)]
+        quantize_pair(nc.vector.tensor_copy, 0, 2)
+        quantize_rest(nc.scalar.copy, 0)
+        first = [project(0, 0, [(128, "a0")]), project(0, 128, [(128, "a1")])]
+        quantize_pair(nc.scalar.copy, 1, 1)
+        quantize_rest(pool_round, 1)
+        first.append(project(0, X_FIRST, [(256, "a2")]))
+        values = [first, [project(1, 0, [(256, "b0"), (256, "b1")])]] + [[project(w, 0, [(T, f"b{w % 2}")])] for w in (2, 3)]
 
-        chunks = [(0, 512), (512, 768), (768, 1024)]
+        chunks = [(0, 256), (256, 768), (768, 1024)]
         grouped = sb.tile([P, U, PACK], BF16, name="grouped", align_bytes=64)
         o_codes = [sb.tile([P, b - a], U32, name=f"o_codes{a}", align_bytes=64) for a, b in chunks]
         o_plane = sb.tile([P, U], U8, name="o_plane", align_bytes=64)
@@ -149,19 +161,7 @@ def tile_picked_wkvput_tanh_lo_kernel(tc, x_words, x_scales, mem, w1, slot, out_
             )
 
         scatter(2)
-        for c0, c1 in ((0, 256), (256, POOL_COLS)):
-            nc.gpsimd.tensor_scalar(
-                out=grouped[:, c0:c1, 2:4],
-                in0=window[2][:, c0:c1].unsqueeze(2).to_broadcast([P, c1 - c0, 2]),
-                scalar1=1.0,
-                scalar2=0.0,
-                op0=MULT,
-                op1=ADD,
-            )
-        nc.scalar.copy(
-            out=grouped[:, POOL_COLS:SPLIT, 2:4],
-            in_=window[2][:, POOL_COLS:SPLIT].unsqueeze(2).to_broadcast([P, SPLIT - POOL_COLS, 2]),
-        )
+        pool_round(grouped[:, 0:SPLIT, 2:4], window[2][:, 0:SPLIT].unsqueeze(2).to_broadcast([P, SPLIT, 2]))
         nc.scalar.copy(out=grouped[:, SPLIT:U, 2], in_=window[2][:, SPLIT:U])
 
         scatter(3)
@@ -172,12 +172,11 @@ def tile_picked_wkvput_tanh_lo_kernel(tc, x_words, x_scales, mem, w1, slot, out_
 
         words_out = out_1[0].rearrange("p n t -> p (n t)").bitcast(I32)
         for g, (c0, c1) in enumerate(chunks):
-            for c in range(c0, c1, 256):
-                nc.vector.quantize_mx(
-                    out=o_codes[g][:, c - c0 : c - c0 + 256].bitcast(FP8X4),
-                    scales=o_plane[:, c : c + 256],
-                    in_=grouped[:, c : c + 256, :].rearrange("p c t -> p (c t)"),
-                )
+            nc.vector.quantize_mx(
+                out=o_codes[g][:].bitcast(FP8X4),
+                scales=o_plane[:, c0:c1],
+                in_=grouped[:, c0:c1, :].rearrange("p c t -> p (c t)"),
+            )
             nc.sync.dma_start(out=words_out[:, c0:c1], in_=o_codes[g][:].bitcast(I32))
         for q in range(QUADS):
             queue = nc.scalar if q % 2 == 0 else nc.sync

@@ -14,6 +14,7 @@ U16 = mybir.dt.uint16
 U8 = mybir.dt.uint8
 FP8X4 = mybir.dt.float8_e4m3fn_x4
 TANH = mybir.ActivationFunctionType.Tanh
+
 MULT = mybir.AluOpType.mult
 ADD = mybir.AluOpType.add
 
@@ -70,7 +71,7 @@ def tile_picked_wkvput_tanh_lo_kernel(tc, x_words, x_scales, mem, w1, slot, out_
 
         def quantize_pair(copy, h, parts):
             n = LH // parts
-            dealt = [sb.tile([P, n, 2, PACK], BF16, name=f"pair_dealt{h}_{i}", align_bytes=64) for i in range(parts)]
+            dealt = [sb.tile([P, n, 2, PACK], BF16, name=f"pair_dealt{h}_{i}", tag=f"dealt{h}_{i}", align_bytes=64) for i in range(parts)]
             for i in range(parts):
                 copy(out=dealt[i][:].rearrange("p l t j -> p l j t"), in_=w_cols(h, 0)[:, i * n : (i + 1) * n])
             for i in range(parts):
@@ -81,15 +82,9 @@ def tile_picked_wkvput_tanh_lo_kernel(tc, x_words, x_scales, mem, w1, slot, out_
                     in_=dealt[i][:].rearrange("p l t j -> p (l t j)"),
                 )
 
-        def pool_round(out, in_):
-            nc.gpsimd.tensor_scalar(out=out, in0=in_, scalar1=1.0, scalar2=0.0, op0=MULT, op1=ADD)
-
-        def quantize_rest(copy, h):
-            dealt = sb.tile([P, 2, LH, PACK], BF16, name=f"rest_dealt{h}", align_bytes=64)
-            if h == 0:
-                copy(out=dealt[:].rearrange("p t l j -> p l j t"), in_=w_cols(h, 2))
-            else:
-                copy(out=dealt[:], in_=w_cols(h, 2).rearrange("p l j t -> p t l j"))
+        def quantize_rest(h, tag):
+            dealt = sb.tile([P, 2, LH, PACK], BF16, name=f"rest_dealt{h}", tag=tag, align_bytes=64)
+            nc.scalar.copy(out=dealt[:].rearrange("p t l j -> p l j t"), in_=w_cols(h, 2))
             for t in range(2):
                 cols = slice(t * P + h * LH, t * P + (h + 1) * LH)
                 nc.vector.quantize_mx(
@@ -124,11 +119,11 @@ def tile_picked_wkvput_tanh_lo_kernel(tc, x_words, x_scales, mem, w1, slot, out_
             return (a, c, y)
 
         quantize_pair(nc.vector.tensor_copy, 0, 2)
-        quantize_rest(nc.scalar.copy, 0)
+        quantize_rest(0, "rest0")
         first = [project(0, 0, [(128, "a0")]), project(0, 128, [(128, "a1")])]
         quantize_pair(nc.scalar.copy, 1, 1)
-        quantize_rest(pool_round, 1)
         first.append(project(0, X_FIRST, [(256, "a2")]))
+        quantize_rest(1, "dealt1_0")
         values = [first, [project(1, 0, [(256, "b0"), (256, "b1")])]] + [[project(w, 0, [(T, f"b{w % 2}")])] for w in (2, 3)]
 
         chunks = [(0, 256), (256, 768), (768, 1024)]
@@ -161,7 +156,14 @@ def tile_picked_wkvput_tanh_lo_kernel(tc, x_words, x_scales, mem, w1, slot, out_
             )
 
         scatter(2)
-        pool_round(grouped[:, 0:SPLIT, 2:4], window[2][:, 0:SPLIT].unsqueeze(2).to_broadcast([P, SPLIT, 2]))
+        nc.gpsimd.tensor_scalar(
+            out=grouped[:, 0:SPLIT, 2:4],
+            in0=window[2][:, 0:SPLIT].unsqueeze(2).to_broadcast([P, SPLIT, 2]),
+            scalar1=1.0,
+            scalar2=0.0,
+            op0=MULT,
+            op1=ADD,
+        )
         nc.scalar.copy(out=grouped[:, SPLIT:U, 2], in_=window[2][:, SPLIT:U])
 
         scatter(3)

@@ -23,8 +23,9 @@ PACK = 4
 QUADS = 4
 HALF = N // 2
 LH = HALF // PACK
-BANK = 512
-SPLIT = 448
+GROUP = 256
+SPLIT = 512
+POOL_FROM = 896
 X_FIRST = 256
 
 
@@ -126,60 +127,60 @@ def tile_picked_wkvput_tanh_lo_kernel(tc, x_words, x_scales, mem, w1, slot, out_
         quantize_rest(1, "dealt1_0")
         values = [first, [project(1, 0, [(256, "b0"), (256, "b1")])]] + [[project(w, 0, [(T, f"b{w % 2}")])] for w in (2, 3)]
 
-        chunks = [(0, 256), (256, 768), (768, 1024)]
+        groups = U // GROUP
         grouped = sb.tile([P, U, PACK], BF16, name="grouped", align_bytes=64)
-        o_codes = [sb.tile([P, b - a], U32, name=f"o_codes{a}", align_bytes=64) for a, b in chunks]
+        stores = [(0, 256, 384), (384, 512, 768), (768, 1024)]
+        o_codes = [sb.tile([P, cuts[-1] - cuts[0]], U32, name=f"o_codes{cuts[0]}", align_bytes=64) for cuts in stores]
         o_plane = sb.tile([P, U], U8, name="o_plane", align_bytes=64)
-        turned = [sb.tile([P, 4, 2, P], BF16, name=f"turned{g}") for g in range(2)]
+        turned = [sb.tile([P, 2, 2, P], BF16, name=f"turned{g}") for g in range(groups)]
 
         def scatter(w):
             for a, b, y in values[w]:
                 nc.vector.tensor_copy(window[w][:].indirect(offsets[:, a // 16 : b // 16]), y[:])
             nc.sync.dma_start(out=rows_of(out_0, w), in_=window[w][:])
 
+        there_banks = [["a0", "a1", "a0", "a1"], ["b0", "b1", "a0", "a1"]]
+        back_banks = ["c0", "c1", "c2", "a2"]
         for w in range(2):
             scatter(w)
-            for g in range(2):
-                bank = ps.tile([P, 4, P], F32, name=f"there{w}_{g}", tag=f"a{g}")
-                for i in range(4):
-                    c = g * BANK + i * P
+            for g in range(groups):
+                bank = ps.tile([P, 2, P], F32, name=f"there{w}_{g}", tag=there_banks[w][g])
+                for i in range(2):
+                    c = g * GROUP + i * P
                     nc.tensor.transpose(bank[:, i, :], window[w][:, c : c + P], identity[:])
                 nc.scalar.copy(out=turned[g][:, :, w, :], in_=bank[:])
-        for g in range(2):
+        for g in range(groups):
             words = turned[g][:].rearrange("p i w q -> p i (w q)").bitcast(F32)
-            bank = ps.tile([P, 4, P], F32, name=f"back{g}", tag=f"c{g}")
-            for i in range(4):
+            bank = ps.tile([P, 2, P], F32, name=f"back{g}", tag=back_banks[g])
+            for i in range(2):
                 nc.tensor.transpose(bank[:, i, :], words[:, i, :], identity[:])
             nc.scalar.copy(
-                out=grouped[:, g * BANK : (g + 1) * BANK, :].bitcast(F32),
-                in_=bank[:].rearrange("p i c -> p (i c)").unsqueeze(2).to_broadcast([P, BANK, 2]),
+                out=grouped[:, g * GROUP : (g + 1) * GROUP, :].bitcast(F32),
+                in_=bank[:].rearrange("p i c -> p (i c)").unsqueeze(2).to_broadcast([P, GROUP, 2]),
             )
+
+        def twice(c0, c1):
+            return window[2][:, c0:c1].unsqueeze(2).to_broadcast([P, c1 - c0, 2])
 
         scatter(2)
-        nc.gpsimd.tensor_scalar(
-            out=grouped[:, 0:SPLIT, 2:4],
-            in0=window[2][:, 0:SPLIT].unsqueeze(2).to_broadcast([P, SPLIT, 2]),
-            scalar1=1.0,
-            scalar2=0.0,
-            op0=MULT,
-            op1=ADD,
-        )
-        nc.scalar.copy(out=grouped[:, SPLIT:U, 2], in_=window[2][:, SPLIT:U])
+        for c0, c1 in ((0, SPLIT), (POOL_FROM, U)):
+            nc.gpsimd.tensor_scalar(out=grouped[:, c0:c1, 2:4], in0=twice(c0, c1), scalar1=1.0, scalar2=0.0, op0=MULT, op1=ADD)
+        nc.scalar.copy(out=grouped[:, SPLIT:POOL_FROM, 2:4], in_=twice(SPLIT, POOL_FROM))
 
         scatter(3)
-        for c0, c1 in ((0, 256), (256, SPLIT)):
-            nc.vector.tensor_copy(out=grouped[:, c0:c1, 3], in_=window[3][:, c0:c1])
-        for c0, c1 in ((SPLIT, 768), (768, U)):
-            nc.scalar.copy(out=grouped[:, c0:c1, 3], in_=window[3][:, c0:c1])
+        for g in range(groups):
+            copy = nc.vector.tensor_copy if (g + 1) * GROUP <= SPLIT else nc.scalar.copy
+            copy(out=grouped[:, g * GROUP : (g + 1) * GROUP, 3], in_=window[3][:, g * GROUP : (g + 1) * GROUP])
 
         words_out = out_1[0].rearrange("p n t -> p (n t)").bitcast(I32)
-        for g, (c0, c1) in enumerate(chunks):
-            nc.vector.quantize_mx(
-                out=o_codes[g][:].bitcast(FP8X4),
-                scales=o_plane[:, c0:c1],
-                in_=grouped[:, c0:c1, :].rearrange("p c t -> p (c t)"),
-            )
-            nc.sync.dma_start(out=words_out[:, c0:c1], in_=o_codes[g][:].bitcast(I32))
+        for codes, cuts in zip(o_codes, stores):
+            for c0, c1 in zip(cuts, cuts[1:]):
+                nc.vector.quantize_mx(
+                    out=codes[:, c0 - cuts[0] : c1 - cuts[0]].bitcast(FP8X4),
+                    scales=o_plane[:, c0:c1],
+                    in_=grouped[:, c0:c1, :].rearrange("p c t -> p (c t)"),
+                )
+            nc.sync.dma_start(out=words_out[:, cuts[0] : cuts[-1]], in_=codes[:].bitcast(I32))
         for q in range(QUADS):
             queue = nc.scalar if q % 2 == 0 else nc.sync
             queue.dma_start(out=out_2[0, 4 * q : 4 * q + 4, :].bitcast(I32), in_=o_plane[32 * q : 32 * q + 4, :].bitcast(I32))

@@ -26,7 +26,8 @@ LH = HALF // PACK
 GROUP = 256
 SPLIT = 512
 POOL_FROM = 896
-X_FIRST = 256
+X_FIRST = 384
+FIRST_CUTS = (0, 128, 288, 512)
 
 
 def tile_picked_wkvput_tanh_lo_kernel(tc, x_words, x_scales, mem, w1, slot, out_0, out_1, out_2):
@@ -100,10 +101,10 @@ def tile_picked_wkvput_tanh_lo_kernel(tc, x_words, x_scales, mem, w1, slot, out_
             cols = slice((w - 2) * P, (w - 1) * P)
             return rest_codes[:, cols], rest_plane[:, cols]
 
-        def project(w, a, parts):
+        values = [sb.tile([P, T], F32, name=f"y{w}") for w in range(PACK)]
+
+        def project(w, c, parts):
             codes, plane = weights(w)
-            y = sb.tile([P, sum(n for n, bank in parts)], F32, name=f"y{w}_{a}")
-            c = a
             for n, bank in parts:
                 acc = ps.tile([P, n], F32, name=f"acc{w}_{c}", tag=bank)
                 nc.tensor.matmul_mx(
@@ -115,17 +116,18 @@ def tile_picked_wkvput_tanh_lo_kernel(tc, x_words, x_scales, mem, w1, slot, out_
                     start=True,
                     stop=True,
                 )
-                nc.scalar.activation(y[:, c - a : c - a + n], acc[:], TANH)
+                nc.scalar.activation(values[w][:, c : c + n], acc[:], TANH)
                 c = c + n
-            return (a, c, y)
 
         quantize_pair(nc.vector.tensor_copy, 0, 2)
         quantize_rest(0, "rest0")
-        first = [project(0, 0, [(128, "a0")]), project(0, 128, [(128, "a1")])]
+        project(0, 0, [(128, "a0"), (256, "a1")])
         quantize_pair(nc.scalar.copy, 1, 1)
-        first.append(project(0, X_FIRST, [(256, "a2")]))
+        project(0, X_FIRST, [(128, "a2")])
         quantize_rest(1, "dealt1_0")
-        values = [first, [project(1, 0, [(256, "b0"), (256, "b1")])]] + [[project(w, 0, [(T, f"b{w % 2}")])] for w in (2, 3)]
+        project(1, 0, [(256, "b0"), (256, "b1")])
+        for w in (2, 3):
+            project(w, 0, [(T, f"b{w % 2}")])
 
         groups = U // GROUP
         grouped = sb.tile([P, U, PACK], BF16, name="grouped", align_bytes=64)
@@ -135,8 +137,9 @@ def tile_picked_wkvput_tanh_lo_kernel(tc, x_words, x_scales, mem, w1, slot, out_
         turned = [sb.tile([P, 2, 2, P], BF16, name=f"turned{g}") for g in range(groups)]
 
         def scatter(w):
-            for a, b, y in values[w]:
-                nc.vector.tensor_copy(window[w][:].indirect(offsets[:, a // 16 : b // 16]), y[:])
+            cuts = FIRST_CUTS if w == 0 else (0, T)
+            for a, b in zip(cuts, cuts[1:]):
+                nc.vector.tensor_copy(window[w][:].indirect(offsets[:, a // 16 : b // 16]), values[w][:, a:b])
             nc.sync.dma_start(out=rows_of(out_0, w), in_=window[w][:])
 
         there_banks = [["a0", "a1", "a0", "a1"], ["b0", "b1", "a0", "a1"]]

@@ -26,7 +26,7 @@ LH = HALF // PACK
 GROUP = 256
 SPLIT = 512
 POOL_FROM = 896
-X_FIRST = 384
+X_FIRST = 320
 FIRST_CUTS = (0, 128, 288, 512)
 
 
@@ -49,8 +49,8 @@ def tile_picked_wkvput_tanh_lo_kernel(tc, x_words, x_scales, mem, w1, slot, out_
         x_rows = x_words[0].rearrange("p n t -> p (n t)").bitcast(I32)
         w_raw = [sb.tile([P, PACK, HALF], F32, name=f"w_raw{h}") for h in range(2)]
         window = [sb.tile([P, U], F32, name=f"window{w}") for w in range(PACK)]
-        nc.sync.dma_start(offsets[:], slot)
         nc.sync.dma_start(out=w_raw[0][:], in_=w_rows[:, :, 0:HALF])
+        nc.sync.dma_start(offsets[:], slot)
         for q in range(QUADS):
             nc.sync.dma_start(out=x_plane[32 * q : 32 * q + 4, :].bitcast(I32), in_=x_scales[0, 4 * q : 4 * q + 4, :].bitcast(I32))
         nc.sync.dma_start(out=x_codes[:, 0:X_FIRST].bitcast(I32), in_=x_rows[:, 0:X_FIRST])
@@ -121,9 +121,9 @@ def tile_picked_wkvput_tanh_lo_kernel(tc, x_words, x_scales, mem, w1, slot, out_
 
         quantize_pair(nc.vector.tensor_copy, 0, 2)
         quantize_rest(0, "rest0")
-        project(0, 0, [(128, "a0"), (256, "a1")])
+        project(0, 0, [(128, "a0"), (128, "a1"), (64, "a2")])
         quantize_pair(nc.scalar.copy, 1, 1)
-        project(0, X_FIRST, [(128, "a2")])
+        project(0, X_FIRST, [(128, "a0"), (64, "a2")])
         quantize_rest(1, "dealt1_0")
         project(1, 0, [(256, "b0"), (256, "b1")])
         for w in (2, 3):

@@ -166,11 +166,11 @@ def tile_picked_wkvput_tanh_lo_kernel(tc, x_words, x_scales, mem, w1, slot, out_
             return window[2][:, c0:c1].unsqueeze(2).to_broadcast([P, c1 - c0, 2])
 
         scatter(2)
-        for c0, c1 in ((0, SPLIT), (POOL_FROM, U)):
-            nc.gpsimd.tensor_scalar(out=grouped[:, c0:c1, 2:4], in0=twice(c0, c1), scalar1=1.0, scalar2=0.0, op0=MULT, op1=ADD)
+        nc.gpsimd.tensor_scalar(out=grouped[:, 0:SPLIT, 2:4], in0=twice(0, SPLIT), scalar1=1.0, scalar2=0.0, op0=MULT, op1=ADD)
         nc.scalar.copy(out=grouped[:, SPLIT:POOL_FROM, 2:4], in_=twice(SPLIT, POOL_FROM))
 
         scatter(3)
+        nc.vector.tensor_copy(out=grouped[:, POOL_FROM:U, 2:4], in_=twice(POOL_FROM, U))
         for g in range(groups):
             copy = nc.vector.tensor_copy if (g + 1) * GROUP <= SPLIT else nc.scalar.copy
             copy(out=grouped[:, g * GROUP : (g + 1) * GROUP, 3], in_=window[3][:, g * GROUP : (g + 1) * GROUP])

@@ -1,7 +1,6 @@
 from contextlib import ExitStack
 
 import concourse.mybir as mybir
-from concourse.masks import make_identity
 
 K, T, N, U = 512, 512, 512, 1024
 FLOPS = 2 * K * T * N
@@ -14,7 +13,7 @@ U16 = mybir.dt.uint16
 U8 = mybir.dt.uint8
 FP8X4 = mybir.dt.float8_e4m3fn_x4
 TANH = mybir.ActivationFunctionType.Tanh
-
+COPY = mybir.ActivationFunctionType.Copy
 MULT = mybir.AluOpType.mult
 ADD = mybir.AluOpType.add
 
@@ -23,11 +22,9 @@ PACK = 4
 QUADS = 4
 HALF = N // 2
 LH = HALF // PACK
-GROUP = 256
-SPLIT = 512
-POOL_FROM = 896
-X_FIRST = 320
-FIRST_CUTS = (0, 128, 288, 512)
+SIDE = U // 2
+CHUNK = 256
+SHARED = 256
 
 
 def tile_picked_wkvput_tanh_lo_kernel(tc, x_words, x_scales, mem, w1, slot, out_0, out_1, out_2):
@@ -40,150 +37,126 @@ def tile_picked_wkvput_tanh_lo_kernel(tc, x_words, x_scales, mem, w1, slot, out_
         x_codes = sb.tile([P, T], U32, name="x_codes", align_bytes=64)
         x_plane = sb.tile([P, T], U8, name="x_plane", align_bytes=64)
 
-        def rows_of(dram, w):
-            if w < 2:
-                return dram.rearrange("(h l t) u -> h l t u", h=2, t=PACK)[w, :, 0:2, :]
-            return dram.rearrange("(p t) u -> p t u", t=PACK)[:, w, :]
+        def rows_of(dram, t):
+            return dram.rearrange("(p t) u -> p t u", t=PACK)[:, t, :]
 
         w_rows = w1.rearrange("(p j) n -> p j n", j=PACK)
         x_rows = x_words[0].rearrange("p n t -> p (n t)").bitcast(I32)
         w_raw = [sb.tile([P, PACK, HALF], F32, name=f"w_raw{h}") for h in range(2)]
-        window = [sb.tile([P, U], F32, name=f"window{w}") for w in range(PACK)]
-        nc.sync.dma_start(out=w_raw[0][:], in_=w_rows[:, :, 0:HALF])
+        window = [sb.tile([P, U], F32, name=f"window{t}") for t in range(PACK)]
+        for h in range(2):
+            nc.sync.dma_start(out=w_raw[h][:], in_=w_rows[:, :, h * HALF : (h + 1) * HALF])
         nc.sync.dma_start(offsets[:], slot)
         for q in range(QUADS):
             nc.sync.dma_start(out=x_plane[32 * q : 32 * q + 4, :].bitcast(I32), in_=x_scales[0, 4 * q : 4 * q + 4, :].bitcast(I32))
-        nc.sync.dma_start(out=x_codes[:, 0:X_FIRST].bitcast(I32), in_=x_rows[:, 0:X_FIRST])
-        nc.sync.dma_start(out=window[0][:], in_=rows_of(mem, 0))
-        nc.sync.dma_start(out=w_raw[1][:], in_=w_rows[:, :, HALF:N])
-        nc.sync.dma_start(out=x_codes[:, X_FIRST:T].bitcast(I32), in_=x_rows[:, X_FIRST:T])
-        for w in range(1, PACK):
-            nc.sync.dma_start(out=window[w][:], in_=rows_of(mem, w))
+        nc.sync.dma_start(out=x_codes[:].bitcast(I32), in_=x_rows)
+        for t in range(PACK):
+            nc.sync.dma_start(out=window[t][:], in_=rows_of(mem, t))
 
-        identity = sb.tile([P, P], F32, name="identity")
-        make_identity(nc, identity[:])
+        w_codes = [sb.tile([P, 2 * P], U32, name=f"w_codes{u}", align_bytes=64) for u in range(2)]
+        w_plane = [sb.tile([P, 2 * P], U8, name=f"w_plane{u}", align_bytes=64) for u in range(2)]
+        dealt = [[sb.tile([P, 2, LH, PACK], BF16, name=f"dealt{u}_{h}", align_bytes=64) for h in range(2)] for u in range(2)]
 
-        pair_codes = [sb.tile([P, P], U32, name=f"pair_codes{h}", align_bytes=64) for h in range(2)]
-        pair_plane = [sb.tile([P, P], U8, name=f"pair_plane{h}", align_bytes=64) for h in range(2)]
-        rest_codes = sb.tile([P, 2 * P], U32, name="rest_codes", align_bytes=64)
-        rest_plane = sb.tile([P, 2 * P], U8, name="rest_plane", align_bytes=64)
+        def deal(copy, u, h):
+            cols = w_raw[h][:].rearrange("p j (l t) -> p l j t", t=PACK)[:, :, :, 2 * u : 2 * u + 2]
+            copy(out=dealt[u][h][:].rearrange("p e l j -> p l j e"), in_=cols)
 
-        def w_cols(h, t0):
-            return w_raw[h][:].rearrange("p j (l t) -> p l j t", t=PACK)[:, :, :, t0 : t0 + 2]
-
-        def quantize_pair(copy, h, parts):
-            n = LH // parts
-            dealt = [sb.tile([P, n, 2, PACK], BF16, name=f"pair_dealt{h}_{i}", tag=f"dealt{h}_{i}", align_bytes=64) for i in range(parts)]
-            for i in range(parts):
-                copy(out=dealt[i][:].rearrange("p l t j -> p l j t"), in_=w_cols(h, 0)[:, i * n : (i + 1) * n])
-            for i in range(parts):
-                cols = slice(2 * i * n, 2 * (i + 1) * n)
+        def quantize_w(u, h):
+            for e in range(2):
+                cols = slice(e * P + h * LH, e * P + (h + 1) * LH)
                 nc.vector.quantize_mx(
-                    out=pair_codes[h][:, cols].bitcast(FP8X4),
-                    scales=pair_plane[h][:, cols],
-                    in_=dealt[i][:].rearrange("p l t j -> p (l t j)"),
+                    out=w_codes[u][:, cols].bitcast(FP8X4),
+                    scales=w_plane[u][:, cols],
+                    in_=dealt[u][h][:, e].rearrange("p l j -> p (l j)"),
                 )
 
-        def quantize_rest(h, tag):
-            dealt = sb.tile([P, 2, LH, PACK], BF16, name=f"rest_dealt{h}", tag=tag, align_bytes=64)
-            nc.scalar.copy(out=dealt[:].rearrange("p t l j -> p l j t"), in_=w_cols(h, 2))
-            for t in range(2):
-                cols = slice(t * P + h * LH, t * P + (h + 1) * LH)
-                nc.vector.quantize_mx(
-                    out=rest_codes[:, cols].bitcast(FP8X4),
-                    scales=rest_plane[:, cols],
-                    in_=dealt[:, t].rearrange("p l j -> p (l j)"),
-                )
+        for h in range(2):
+            deal(nc.vector.tensor_copy, 0, h)
+            deal(nc.scalar.copy, 1, h)
+            quantize_w(0, h)
+            quantize_w(1, h)
 
-        def weights(w):
-            if w < 2:
-                return pair_codes[w][:], pair_plane[w][:]
-            cols = slice((w - 2) * P, (w - 1) * P)
-            return rest_codes[:, cols], rest_plane[:, cols]
+        values = [sb.tile([P, T], F32, name=f"y{t}") for t in range(PACK)]
 
-        values = [sb.tile([P, T], F32, name=f"y{w}") for w in range(PACK)]
-
-        def project(w, c, parts):
-            codes, plane = weights(w)
-            for n, bank in parts:
-                acc = ps.tile([P, n], F32, name=f"acc{w}_{c}", tag=bank)
+        def project(t, cuts):
+            cols = slice((t % 2) * P, (t % 2 + 1) * P)
+            for a, b in zip(cuts, cuts[1:]):
+                acc = ps.tile([P, b - a], F32, name=f"acc{t}_{a}")
                 nc.tensor.matmul_mx(
                     out=acc[:],
-                    lhsT=codes.bitcast(FP8X4),
-                    lhsT_scale=plane,
-                    rhs=x_codes[:, c : c + n].bitcast(FP8X4),
-                    rhs_scale=x_plane[:, c : c + n],
+                    lhsT=w_codes[t // 2][:, cols].bitcast(FP8X4),
+                    lhsT_scale=w_plane[t // 2][:, cols],
+                    rhs=x_codes[:, a:b].bitcast(FP8X4),
+                    rhs_scale=x_plane[:, a:b],
                     start=True,
                     stop=True,
                 )
-                nc.scalar.activation(values[w][:, c : c + n], acc[:], TANH)
-                c = c + n
+                nc.scalar.activation(values[t][:, a:b], acc[:], TANH)
 
-        quantize_pair(nc.vector.tensor_copy, 0, 2)
-        quantize_rest(0, "rest0")
-        project(0, 0, [(128, "a0"), (128, "a1"), (64, "a2")])
-        quantize_pair(nc.scalar.copy, 1, 1)
-        project(0, X_FIRST, [(128, "a0"), (64, "a2")])
-        quantize_rest(1, "dealt1_0")
-        project(1, 0, [(256, "b0"), (256, "b1")])
-        for w in (2, 3):
-            project(w, 0, [(T, f"b{w % 2}")])
+        project(0, (0, 128, 256, T))
+        for t in range(1, PACK):
+            project(t, (0, T))
 
-        groups = U // GROUP
-        grouped = sb.tile([P, U, PACK], BF16, name="grouped", align_bytes=64)
-        stores = [(0, 256, 384), (384, 512, 768), (768, 1024)]
-        o_codes = [sb.tile([P, cuts[-1] - cuts[0]], U32, name=f"o_codes{cuts[0]}", align_bytes=64) for cuts in stores]
+        def vector_scatter(t, a, b):
+            nc.vector.tensor_copy(window[t][:].indirect(offsets[:, a // 16 : b // 16]), values[t][:, a:b])
+
+        def scalar_scatter(t, a, b):
+            nc.scalar.activation(window[t][:].indirect(offsets[:, a // 16 : b // 16]), values[t][:, a:b], COPY)
+
+        def store(t):
+            nc.sync.dma_start(out=rows_of(out_0, t), in_=window[t][:])
+
+        pairs = [sb.tile([P, 2, SIDE, 2], BF16, name=f"pairs{s}") for s in range(2)]
+
+        def side(t, s):
+            return window[t][:, s * SIDE : (s + 1) * SIDE]
+
+        def gpsimd_round(out, in_):
+            nc.gpsimd.tensor_scalar(out=out, in0=in_, scalar1=1.0, scalar2=0.0, op0=MULT, op1=ADD)
+
+        for a, b in ((0, 128), (128, 256), (256, T)):
+            vector_scatter(0, a, b)
+        store(0)
+        for s in range(2):
+            gpsimd_round(pairs[s][:, 0, :, 0], side(0, s))
+
+        for a, b in ((0, T // 2), (T // 2, T)):
+            scalar_scatter(1, a, b)
+        store(1)
+        for s in range(2):
+            gpsimd_round(pairs[s][:, 0, :, 1], side(1, s))
+
+        vector_scatter(2, 0, SHARED)
+        scalar_scatter(2, SHARED, T)
+        store(2)
+        gpsimd_round(pairs[0][:, 1], side(2, 0).unsqueeze(2).to_broadcast([P, SIDE, 2]))
+        nc.scalar.copy(out=pairs[1][:, 1, :, 0], in_=side(2, 1))
+
+        vector_scatter(3, 0, T)
+        store(3)
+        nc.vector.tensor_copy(out=pairs[0][:, 1, :, 1], in_=side(3, 0))
+        nc.scalar.copy(out=pairs[1][:, 1, :, 1], in_=side(3, 1))
+
+        chunks = U // CHUNK
+        grouped = [sb.tile([P, CHUNK, PACK], BF16, name=f"grouped{g}", align_bytes=64) for g in range(chunks)]
+        for g in range(chunks):
+            s, c = divmod(g * CHUNK, SIDE)
+            copy, word = (nc.vector.tensor_copy, I32) if s == 0 else (nc.scalar.copy, U32)
+            words = pairs[s][:].rearrange("p u c e -> p u (c e)").bitcast(word)
+            copy(out=grouped[g][:].bitcast(word), in_=words[:, :, c : c + CHUNK].rearrange("p u c -> p c u"))
+
+        stores = [(0, 2), (2, 3), (3, 4)]
+        o_codes = [sb.tile([P, (b - a) * CHUNK], U32, name=f"o_codes{a}", align_bytes=64) for a, b in stores]
         o_plane = sb.tile([P, U], U8, name="o_plane", align_bytes=64)
-        turned = [sb.tile([P, 2, 2, P], BF16, name=f"turned{g}") for g in range(groups)]
-
-        def scatter(w):
-            cuts = FIRST_CUTS if w == 0 else (0, T)
-            for a, b in zip(cuts, cuts[1:]):
-                nc.vector.tensor_copy(window[w][:].indirect(offsets[:, a // 16 : b // 16]), values[w][:, a:b])
-            nc.sync.dma_start(out=rows_of(out_0, w), in_=window[w][:])
-
-        there_banks = [["a0", "a1", "a0", "a1"], ["b0", "b1", "a0", "a1"]]
-        back_banks = ["c0", "c1", "c2", "a2"]
-        for w in range(2):
-            scatter(w)
-            for g in range(groups):
-                bank = ps.tile([P, 2, P], F32, name=f"there{w}_{g}", tag=there_banks[w][g])
-                for i in range(2):
-                    c = g * GROUP + i * P
-                    nc.tensor.transpose(bank[:, i, :], window[w][:, c : c + P], identity[:])
-                nc.scalar.copy(out=turned[g][:, :, w, :], in_=bank[:])
-        for g in range(groups):
-            words = turned[g][:].rearrange("p i w q -> p i (w q)").bitcast(F32)
-            bank = ps.tile([P, 2, P], F32, name=f"back{g}", tag=back_banks[g])
-            for i in range(2):
-                nc.tensor.transpose(bank[:, i, :], words[:, i, :], identity[:])
-            nc.scalar.copy(
-                out=grouped[:, g * GROUP : (g + 1) * GROUP, :].bitcast(F32),
-                in_=bank[:].rearrange("p i c -> p (i c)").unsqueeze(2).to_broadcast([P, GROUP, 2]),
-            )
-
-        def twice(c0, c1):
-            return window[2][:, c0:c1].unsqueeze(2).to_broadcast([P, c1 - c0, 2])
-
-        scatter(2)
-        nc.gpsimd.tensor_scalar(out=grouped[:, 0:SPLIT, 2:4], in0=twice(0, SPLIT), scalar1=1.0, scalar2=0.0, op0=MULT, op1=ADD)
-        nc.scalar.copy(out=grouped[:, SPLIT:POOL_FROM, 2:4], in_=twice(SPLIT, POOL_FROM))
-
-        scatter(3)
-        nc.vector.tensor_copy(out=grouped[:, POOL_FROM:U, 2:4], in_=twice(POOL_FROM, U))
-        for g in range(groups):
-            copy = nc.vector.tensor_copy if (g + 1) * GROUP <= SPLIT else nc.scalar.copy
-            copy(out=grouped[:, g * GROUP : (g + 1) * GROUP, 3], in_=window[3][:, g * GROUP : (g + 1) * GROUP])
-
         words_out = out_1[0].rearrange("p n t -> p (n t)").bitcast(I32)
-        for codes, cuts in zip(o_codes, stores):
-            for c0, c1 in zip(cuts, cuts[1:]):
+        for codes, (a, b) in zip(o_codes, stores):
+            for g in range(a, b):
                 nc.vector.quantize_mx(
-                    out=codes[:, c0 - cuts[0] : c1 - cuts[0]].bitcast(FP8X4),
-                    scales=o_plane[:, c0:c1],
-                    in_=grouped[:, c0:c1, :].rearrange("p c t -> p (c t)"),
+                    out=codes[:, (g - a) * CHUNK : (g - a + 1) * CHUNK].bitcast(FP8X4),
+                    scales=o_plane[:, g * CHUNK : (g + 1) * CHUNK],
+                    in_=grouped[g][:].rearrange("p c t -> p (c t)"),
                 )
-            nc.sync.dma_start(out=words_out[:, cuts[0] : cuts[-1]], in_=codes[:].bitcast(I32))
+            nc.sync.dma_start(out=words_out[:, a * CHUNK : b * CHUNK], in_=codes[:].bitcast(I32))
         for q in range(QUADS):
             queue = nc.scalar if q % 2 == 0 else nc.sync
             queue.dma_start(out=out_2[0, 4 * q : 4 * q + 4, :].bitcast(I32), in_=o_plane[32 * q : 32 * q + 4, :].bitcast(I32))

@@ -22,9 +22,9 @@ PACK = 4
 QUADS = 4
 HALF = N // 2
 LH = HALF // PACK
-SIDE = U // 2
-CHUNK = 256
+TH = T // 2
 SHARED = 256
+SPLIT = 512
 
 
 def tile_picked_wkvput_tanh_lo_kernel(tc, x_words, x_scales, mem, w1, slot, out_0, out_1, out_2):
@@ -46,11 +46,13 @@ def tile_picked_wkvput_tanh_lo_kernel(tc, x_words, x_scales, mem, w1, slot, out_
         window = [sb.tile([P, U], F32, name=f"window{t}") for t in range(PACK)]
         for h in range(2):
             nc.sync.dma_start(out=w_raw[h][:], in_=w_rows[:, :, h * HALF : (h + 1) * HALF])
-        nc.sync.dma_start(offsets[:], slot)
         for q in range(QUADS):
             nc.sync.dma_start(out=x_plane[32 * q : 32 * q + 4, :].bitcast(I32), in_=x_scales[0, 4 * q : 4 * q + 4, :].bitcast(I32))
-        nc.sync.dma_start(out=x_codes[:].bitcast(I32), in_=x_rows)
-        for t in range(PACK):
+        nc.sync.dma_start(out=x_codes[:, 0:TH].bitcast(I32), in_=x_rows[:, 0:TH])
+        nc.sync.dma_start(out=window[0][:], in_=rows_of(mem, 0))
+        nc.sync.dma_start(offsets[:], slot)
+        nc.sync.dma_start(out=x_codes[:, TH:T].bitcast(I32), in_=x_rows[:, TH:T])
+        for t in range(1, PACK):
             nc.sync.dma_start(out=window[t][:], in_=rows_of(mem, t))
 
         w_codes = [sb.tile([P, 2 * P], U32, name=f"w_codes{u}", align_bytes=64) for u in range(2)]
@@ -78,24 +80,19 @@ def tile_picked_wkvput_tanh_lo_kernel(tc, x_words, x_scales, mem, w1, slot, out_
 
         values = [sb.tile([P, T], F32, name=f"y{t}") for t in range(PACK)]
 
-        def project(t, cuts):
+        def project(t, a, b):
             cols = slice((t % 2) * P, (t % 2 + 1) * P)
-            for a, b in zip(cuts, cuts[1:]):
-                acc = ps.tile([P, b - a], F32, name=f"acc{t}_{a}")
-                nc.tensor.matmul_mx(
-                    out=acc[:],
-                    lhsT=w_codes[t // 2][:, cols].bitcast(FP8X4),
-                    lhsT_scale=w_plane[t // 2][:, cols],
-                    rhs=x_codes[:, a:b].bitcast(FP8X4),
-                    rhs_scale=x_plane[:, a:b],
-                    start=True,
-                    stop=True,
-                )
-                nc.scalar.activation(values[t][:, a:b], acc[:], TANH)
-
-        project(0, (0, 128, 256, T))
-        for t in range(1, PACK):
-            project(t, (0, T))
+            acc = ps.tile([P, b - a], F32, name=f"acc{t}_{a}")
+            nc.tensor.matmul_mx(
+                out=acc[:],
+                lhsT=w_codes[t // 2][:, cols].bitcast(FP8X4),
+                lhsT_scale=w_plane[t // 2][:, cols],
+                rhs=x_codes[:, a:b].bitcast(FP8X4),
+                rhs_scale=x_plane[:, a:b],
+                start=True,
+                stop=True,
+            )
+            nc.scalar.activation(values[t][:, a:b], acc[:], TANH)
 
         def vector_scatter(t, a, b):
             nc.vector.tensor_copy(window[t][:].indirect(offsets[:, a // 16 : b // 16]), values[t][:, a:b])
@@ -106,22 +103,30 @@ def tile_picked_wkvput_tanh_lo_kernel(tc, x_words, x_scales, mem, w1, slot, out_
         def store(t):
             nc.sync.dma_start(out=rows_of(out_0, t), in_=window[t][:])
 
-        pairs = [sb.tile([P, 2, SIDE, 2], BF16, name=f"pairs{s}") for s in range(2)]
+        sides = [(0, SPLIT), (SPLIT, U)]
+        pairs = [sb.tile([P, 2, b - a, 2], BF16, name=f"pairs{a}") for a, b in sides]
 
         def side(t, s):
-            return window[t][:, s * SIDE : (s + 1) * SIDE]
+            return window[t][:, sides[s][0] : sides[s][1]]
 
         def gpsimd_round(out, in_):
             nc.gpsimd.tensor_scalar(out=out, in0=in_, scalar1=1.0, scalar2=0.0, op0=MULT, op1=ADD)
 
-        for a, b in ((0, 128), (128, 256), (256, T)):
-            vector_scatter(0, a, b)
+        for t in range(PACK):
+            project(t, 0, TH)
+        project(0, TH, T)
+        project(1, TH, T)
+
+        vector_scatter(0, 0, TH)
+        vector_scatter(0, TH, T)
         store(0)
         for s in range(2):
             gpsimd_round(pairs[s][:, 0, :, 0], side(0, s))
 
-        for a, b in ((0, T // 2), (T // 2, T)):
-            scalar_scatter(1, a, b)
+        scalar_scatter(1, 0, TH)
+        project(2, TH, T)
+        project(3, TH, T)
+        scalar_scatter(1, TH, T)
         store(1)
         for s in range(2):
             gpsimd_round(pairs[s][:, 0, :, 1], side(1, s))
@@ -129,34 +134,31 @@ def tile_picked_wkvput_tanh_lo_kernel(tc, x_words, x_scales, mem, w1, slot, out_
         vector_scatter(2, 0, SHARED)
         scalar_scatter(2, SHARED, T)
         store(2)
-        gpsimd_round(pairs[0][:, 1], side(2, 0).unsqueeze(2).to_broadcast([P, SIDE, 2]))
+        gpsimd_round(pairs[0][:, 1], side(2, 0).unsqueeze(2).to_broadcast([P, SPLIT, 2]))
         nc.scalar.copy(out=pairs[1][:, 1, :, 0], in_=side(2, 1))
 
         vector_scatter(3, 0, T)
         store(3)
-        nc.vector.tensor_copy(out=pairs[0][:, 1, :, 1], in_=side(3, 0))
-        nc.scalar.copy(out=pairs[1][:, 1, :, 1], in_=side(3, 1))
-
-        chunks = U // CHUNK
-        grouped = [sb.tile([P, CHUNK, PACK], BF16, name=f"grouped{g}", align_bytes=64) for g in range(chunks)]
-        for g in range(chunks):
-            s, c = divmod(g * CHUNK, SIDE)
-            copy, word = (nc.vector.tensor_copy, I32) if s == 0 else (nc.scalar.copy, U32)
+        grouped = {}
+        for s, cuts, copy, word in ((0, (0, 256, 512), nc.vector.tensor_copy, I32), (1, (512, 768, 1024), nc.scalar.copy, U32)):
             words = pairs[s][:].rearrange("p u c e -> p u (c e)").bitcast(word)
-            copy(out=grouped[g][:].bitcast(word), in_=words[:, :, c : c + CHUNK].rearrange("p u c -> p c u"))
+            for a, b in zip(cuts, cuts[1:]):
+                copy(out=pairs[s][:, 1, a - cuts[0] : b - cuts[0], 1], in_=window[3][:, a:b])
+            for a, b in zip(cuts, cuts[1:]):
+                grouped[a] = sb.tile([P, b - a, PACK], BF16, name=f"grouped{a}", align_bytes=64)
+                copy(out=grouped[a][:].bitcast(word), in_=words[:, :, a - cuts[0] : b - cuts[0]].rearrange("p u c -> p c u"))
 
-        stores = [(0, 2), (2, 3), (3, 4)]
-        o_codes = [sb.tile([P, (b - a) * CHUNK], U32, name=f"o_codes{a}", align_bytes=64) for a, b in stores]
         o_plane = sb.tile([P, U], U8, name="o_plane", align_bytes=64)
         words_out = out_1[0].rearrange("p n t -> p (n t)").bitcast(I32)
-        for codes, (a, b) in zip(o_codes, stores):
-            for g in range(a, b):
+        for cuts in [(0, 256, 512), (512, 768), (768, 1024)]:
+            codes = sb.tile([P, cuts[-1] - cuts[0]], U32, name=f"o_codes{cuts[0]}", align_bytes=64)
+            for a, b in zip(cuts, cuts[1:]):
                 nc.vector.quantize_mx(
-                    out=codes[:, (g - a) * CHUNK : (g - a + 1) * CHUNK].bitcast(FP8X4),
-                    scales=o_plane[:, g * CHUNK : (g + 1) * CHUNK],
-                    in_=grouped[g][:].rearrange("p c t -> p (c t)"),
+                    out=codes[:, a - cuts[0] : b - cuts[0]].bitcast(FP8X4),
+                    scales=o_plane[:, a:b],
+                    in_=grouped[a][:].rearrange("p c t -> p (c t)"),
                 )
-            nc.sync.dma_start(out=words_out[:, a * CHUNK : b * CHUNK], in_=codes[:].bitcast(I32))
+            nc.sync.dma_start(out=words_out[:, cuts[0] : cuts[-1]], in_=codes[:].bitcast(I32))
         for q in range(QUADS):
             queue = nc.scalar if q % 2 == 0 else nc.sync
             queue.dma_start(out=out_2[0, 4 * q : 4 * q + 4, :].bitcast(I32), in_=o_plane[32 * q : 32 * q + 4, :].bitcast(I32))

@@ -23,8 +23,9 @@ QUADS = 4
 HALF = N // 2
 LH = HALF // PACK
 TH = T // 2
-SHARED = 256
+SHARED = 224
 SPLIT = 512
+POOL_COLS = 384
 
 
 def tile_picked_wkvput_tanh_lo_kernel(tc, x_words, x_scales, mem, w1, slot, out_0, out_1, out_2):
@@ -48,10 +49,9 @@ def tile_picked_wkvput_tanh_lo_kernel(tc, x_words, x_scales, mem, w1, slot, out_
             nc.sync.dma_start(out=w_raw[h][:], in_=w_rows[:, :, h * HALF : (h + 1) * HALF])
         for q in range(QUADS):
             nc.sync.dma_start(out=x_plane[32 * q : 32 * q + 4, :].bitcast(I32), in_=x_scales[0, 4 * q : 4 * q + 4, :].bitcast(I32))
-        nc.sync.dma_start(out=x_codes[:, 0:TH].bitcast(I32), in_=x_rows[:, 0:TH])
+        nc.sync.dma_start(out=x_codes[:].bitcast(I32), in_=x_rows)
         nc.sync.dma_start(out=window[0][:], in_=rows_of(mem, 0))
         nc.sync.dma_start(offsets[:], slot)
-        nc.sync.dma_start(out=x_codes[:, TH:T].bitcast(I32), in_=x_rows[:, TH:T])
         for t in range(1, PACK):
             nc.sync.dma_start(out=window[t][:], in_=rows_of(mem, t))
 
@@ -103,50 +103,48 @@ def tile_picked_wkvput_tanh_lo_kernel(tc, x_words, x_scales, mem, w1, slot, out_
         def store(t):
             nc.sync.dma_start(out=rows_of(out_0, t), in_=window[t][:])
 
-        sides = [(0, SPLIT), (SPLIT, U)]
-        pairs = [sb.tile([P, 2, b - a, 2], BF16, name=f"pairs{a}") for a, b in sides]
+        pair_words = sb.tile([P, 2 * U], F32, name="pair_words")
+        pairs = pair_words[:].bitcast(BF16).rearrange("p (u c e) -> p u c e", u=2, e=2)
 
-        def side(t, s):
-            return window[t][:, sides[s][0] : sides[s][1]]
+        def twice(a, b):
+            return window[2][:, a:b].unsqueeze(2).to_broadcast([P, b - a, 2])
 
         def gpsimd_round(out, in_):
             nc.gpsimd.tensor_scalar(out=out, in0=in_, scalar1=1.0, scalar2=0.0, op0=MULT, op1=ADD)
 
-        for t in range(PACK):
-            project(t, 0, TH)
+        project(0, 0, TH)
         project(0, TH, T)
-        project(1, TH, T)
+        project(1, 0, T)
+        project(2, 0, T)
 
         vector_scatter(0, 0, TH)
         vector_scatter(0, TH, T)
         store(0)
-        for s in range(2):
-            gpsimd_round(pairs[s][:, 0, :, 0], side(0, s))
+        gpsimd_round(pairs[:, 0, :, 0], window[0][:])
 
         scalar_scatter(1, 0, TH)
-        project(2, TH, T)
-        project(3, TH, T)
+        project(3, 0, T)
         scalar_scatter(1, TH, T)
         store(1)
-        for s in range(2):
-            gpsimd_round(pairs[s][:, 0, :, 1], side(1, s))
+        gpsimd_round(pairs[:, 0, :, 1], window[1][:])
 
         vector_scatter(2, 0, SHARED)
         scalar_scatter(2, SHARED, T)
         store(2)
-        gpsimd_round(pairs[0][:, 1], side(2, 0).unsqueeze(2).to_broadcast([P, SPLIT, 2]))
-        nc.scalar.copy(out=pairs[1][:, 1, :, 0], in_=side(2, 1))
+        gpsimd_round(pairs[:, 1, 0:POOL_COLS], twice(0, POOL_COLS))
+        nc.scalar.copy(out=pairs[:, 1, POOL_COLS:SPLIT], in_=twice(POOL_COLS, SPLIT))
+        nc.scalar.copy(out=pairs[:, 1, SPLIT:U, 0], in_=window[2][:, SPLIT:U])
 
         vector_scatter(3, 0, T)
         store(3)
         grouped = {}
-        for s, cuts, copy, word in ((0, (0, 256, 512), nc.vector.tensor_copy, I32), (1, (512, 768, 1024), nc.scalar.copy, U32)):
-            words = pairs[s][:].rearrange("p u c e -> p u (c e)").bitcast(word)
+        for cuts, copy, word in (((0, 256, 512), nc.vector.tensor_copy, I32), ((512, 768, 1024), nc.scalar.copy, U32)):
+            words = pair_words[:].bitcast(word).rearrange("p (u c) -> p c u", u=2)
             for a, b in zip(cuts, cuts[1:]):
-                copy(out=pairs[s][:, 1, a - cuts[0] : b - cuts[0], 1], in_=window[3][:, a:b])
+                copy(out=pairs[:, 1, a:b, 1], in_=window[3][:, a:b])
             for a, b in zip(cuts, cuts[1:]):
                 grouped[a] = sb.tile([P, b - a, PACK], BF16, name=f"grouped{a}", align_bytes=64)
-                copy(out=grouped[a][:].bitcast(word), in_=words[:, :, a - cuts[0] : b - cuts[0]].rearrange("p u c -> p c u"))
+                copy(out=grouped[a][:].bitcast(word), in_=words[:, a:b, :])
 
         o_plane = sb.tile([P, U], U8, name="o_plane", align_bytes=64)
         words_out = out_1[0].rearrange("p n t -> p (n t)").bitcast(I32)

@@ -23,8 +23,8 @@ QUADS = 4
 HALF = N // 2
 LH = HALF // PACK
 TH = T // 2
-SHARED = 224
-SPLIT = 512
+SHARED = 192
+SPLIT = 576
 POOL_COLS = 384
 
 
@@ -49,9 +49,10 @@ def tile_picked_wkvput_tanh_lo_kernel(tc, x_words, x_scales, mem, w1, slot, out_
             nc.sync.dma_start(out=w_raw[h][:], in_=w_rows[:, :, h * HALF : (h + 1) * HALF])
         for q in range(QUADS):
             nc.sync.dma_start(out=x_plane[32 * q : 32 * q + 4, :].bitcast(I32), in_=x_scales[0, 4 * q : 4 * q + 4, :].bitcast(I32))
-        nc.sync.dma_start(out=x_codes[:].bitcast(I32), in_=x_rows)
+        nc.sync.dma_start(out=x_codes[:, 0:TH].bitcast(I32), in_=x_rows[:, 0:TH])
         nc.sync.dma_start(out=window[0][:], in_=rows_of(mem, 0))
         nc.sync.dma_start(offsets[:], slot)
+        nc.sync.dma_start(out=x_codes[:, TH:T].bitcast(I32), in_=x_rows[:, TH:T])
         for t in range(1, PACK):
             nc.sync.dma_start(out=window[t][:], in_=rows_of(mem, t))
 
@@ -112,10 +113,10 @@ def tile_picked_wkvput_tanh_lo_kernel(tc, x_words, x_scales, mem, w1, slot, out_
         def gpsimd_round(out, in_):
             nc.gpsimd.tensor_scalar(out=out, in0=in_, scalar1=1.0, scalar2=0.0, op0=MULT, op1=ADD)
 
-        project(0, 0, TH)
+        for t in range(PACK):
+            project(t, 0, TH)
         project(0, TH, T)
-        project(1, 0, T)
-        project(2, 0, T)
+        project(1, TH, T)
 
         vector_scatter(0, 0, TH)
         vector_scatter(0, TH, T)
@@ -123,8 +124,9 @@ def tile_picked_wkvput_tanh_lo_kernel(tc, x_words, x_scales, mem, w1, slot, out_
         gpsimd_round(pairs[:, 0, :, 0], window[0][:])
 
         scalar_scatter(1, 0, TH)
-        project(3, 0, T)
+        project(3, TH, T)
         scalar_scatter(1, TH, T)
+        project(2, TH, T)
         store(1)
         gpsimd_round(pairs[:, 0, :, 1], window[1][:])
 
@@ -137,14 +139,13 @@ def tile_picked_wkvput_tanh_lo_kernel(tc, x_words, x_scales, mem, w1, slot, out_
 
         vector_scatter(3, 0, T)
         store(3)
-        grouped = {}
-        for cuts, copy, word in (((0, 256, 512), nc.vector.tensor_copy, I32), ((512, 768, 1024), nc.scalar.copy, U32)):
+        grouped = sb.tile([P, U, PACK], BF16, name="grouped", align_bytes=64)
+        for cuts, copy, word in (((0, 256, SPLIT), nc.vector.tensor_copy, I32), ((SPLIT, 768, U), nc.scalar.copy, U32)):
             words = pair_words[:].bitcast(word).rearrange("p (u c) -> p c u", u=2)
             for a, b in zip(cuts, cuts[1:]):
                 copy(out=pairs[:, 1, a:b, 1], in_=window[3][:, a:b])
             for a, b in zip(cuts, cuts[1:]):
-                grouped[a] = sb.tile([P, b - a, PACK], BF16, name=f"grouped{a}", align_bytes=64)
-                copy(out=grouped[a][:].bitcast(word), in_=words[:, a:b, :])
+                copy(out=grouped[:, a:b, :].bitcast(word), in_=words[:, a:b, :])
 
         o_plane = sb.tile([P, U], U8, name="o_plane", align_bytes=64)
         words_out = out_1[0].rearrange("p n t -> p (n t)").bitcast(I32)
@@ -154,7 +155,7 @@ def tile_picked_wkvput_tanh_lo_kernel(tc, x_words, x_scales, mem, w1, slot, out_
                 nc.vector.quantize_mx(
                     out=codes[:, a - cuts[0] : b - cuts[0]].bitcast(FP8X4),
                     scales=o_plane[:, a:b],
-                    in_=grouped[a][:].rearrange("p c t -> p (c t)"),
+                    in_=grouped[:, a:b, :].rearrange("p c t -> p (c t)"),
                 )
             nc.sync.dma_start(out=words_out[:, cuts[0] : cuts[-1]], in_=codes[:].bitcast(I32))
         for q in range(QUADS):

@@ -45,13 +45,13 @@ def tile_picked_wkvput_tanh_lo_kernel(tc, x_words, x_scales, mem, w1, slot, out_
         x_rows = x_words[0].rearrange("p n t -> p (n t)").bitcast(I32)
         w_raw = [sb.tile([P, PACK, HALF], F32, name=f"w_raw{h}") for h in range(2)]
         window = [sb.tile([P, U], F32, name=f"window{t}") for t in range(PACK)]
+        nc.sync.dma_start(offsets[:], slot)
         for h in range(2):
             nc.sync.dma_start(out=w_raw[h][:], in_=w_rows[:, :, h * HALF : (h + 1) * HALF])
         for q in range(QUADS):
             nc.sync.dma_start(out=x_plane[32 * q : 32 * q + 4, :].bitcast(I32), in_=x_scales[0, 4 * q : 4 * q + 4, :].bitcast(I32))
         nc.sync.dma_start(out=x_codes[:, 0:TH].bitcast(I32), in_=x_rows[:, 0:TH])
         nc.sync.dma_start(out=window[0][:], in_=rows_of(mem, 0))
-        nc.sync.dma_start(offsets[:], slot)
         nc.sync.dma_start(out=x_codes[:, TH:T].bitcast(I32), in_=x_rows[:, TH:T])
         for t in range(1, PACK):
             nc.sync.dma_start(out=window[t][:], in_=rows_of(mem, t))
@@ -124,9 +124,9 @@ def tile_picked_wkvput_tanh_lo_kernel(tc, x_words, x_scales, mem, w1, slot, out_
         gpsimd_round(pairs[:, 0, :, 0], window[0][:])
 
         scalar_scatter(1, 0, TH)
+        project(2, TH, T)
         project(3, TH, T)
         scalar_scatter(1, TH, T)
-        project(2, TH, T)
         store(1)
         gpsimd_round(pairs[:, 0, :, 1], window[1][:])
 
@@ -149,7 +149,7 @@ def tile_picked_wkvput_tanh_lo_kernel(tc, x_words, x_scales, mem, w1, slot, out_
 
         o_plane = sb.tile([P, U], U8, name="o_plane", align_bytes=64)
         words_out = out_1[0].rearrange("p n t -> p (n t)").bitcast(I32)
-        for cuts in [(0, 256, 512), (512, 768), (768, 1024)]:
+        for cuts in [(0, 256), (256, 512), (512, 768), (768, 1024)]:
             codes = sb.tile([P, cuts[-1] - cuts[0]], U32, name=f"o_codes{cuts[0]}", align_bytes=64)
             for a, b in zip(cuts, cuts[1:]):
                 nc.vector.quantize_mx(

@@ -23,7 +23,7 @@ QUADS = 4
 HALF = N // 2
 LH = HALF // PACK
 TH = T // 2
-SHARED = 192
+SHARED = 160
 SPLIT = 576
 POOL_COLS = 384
 
@@ -45,13 +45,18 @@ def tile_picked_wkvput_tanh_lo_kernel(tc, x_words, x_scales, mem, w1, slot, out_
         x_rows = x_words[0].rearrange("p n t -> p (n t)").bitcast(I32)
         w_raw = [sb.tile([P, PACK, HALF], F32, name=f"w_raw{h}") for h in range(2)]
         window = [sb.tile([P, U], F32, name=f"window{t}") for t in range(PACK)]
-        nc.sync.dma_start(offsets[:], slot)
+
+        def load_scales(q):
+            nc.sync.dma_start(out=x_plane[32 * q : 32 * q + 4, :].bitcast(I32), in_=x_scales[0, 4 * q : 4 * q + 4, :].bitcast(I32))
+
         for h in range(2):
             nc.sync.dma_start(out=w_raw[h][:], in_=w_rows[:, :, h * HALF : (h + 1) * HALF])
-        for q in range(QUADS):
-            nc.sync.dma_start(out=x_plane[32 * q : 32 * q + 4, :].bitcast(I32), in_=x_scales[0, 4 * q : 4 * q + 4, :].bitcast(I32))
+            load_scales(h)
+        for q in range(2, QUADS):
+            load_scales(q)
         nc.sync.dma_start(out=x_codes[:, 0:TH].bitcast(I32), in_=x_rows[:, 0:TH])
         nc.sync.dma_start(out=window[0][:], in_=rows_of(mem, 0))
+        nc.sync.dma_start(offsets[:], slot)
         nc.sync.dma_start(out=x_codes[:, TH:T].bitcast(I32), in_=x_rows[:, TH:T])
         for t in range(1, PACK):
             nc.sync.dma_start(out=window[t][:], in_=rows_of(mem, t))
@@ -149,7 +154,7 @@ def tile_picked_wkvput_tanh_lo_kernel(tc, x_words, x_scales, mem, w1, slot, out_
 
         o_plane = sb.tile([P, U], U8, name="o_plane", align_bytes=64)
         words_out = out_1[0].rearrange("p n t -> p (n t)").bitcast(I32)
-        for cuts in [(0, 256), (256, 512), (512, 768), (768, 1024)]:
+        for cuts in [(0, 256, 512), (512, 768), (768, 1024)]:
             codes = sb.tile([P, cuts[-1] - cuts[0]], U32, name=f"o_codes{cuts[0]}", align_bytes=64)
             for a, b in zip(cuts, cuts[1:]):
                 nc.vector.quantize_mx(

@@ -23,8 +23,9 @@ QUADS = 4
 HALF = N // 2
 LH = HALF // PACK
 TH = T // 2
-SHARED = 160
+SHARED = 192
 SPLIT = 576
+DEAL_FIRST = 40
 POOL_COLS = 384
 
 
@@ -65,9 +66,9 @@ def tile_picked_wkvput_tanh_lo_kernel(tc, x_words, x_scales, mem, w1, slot, out_
         w_plane = [sb.tile([P, 2 * P], U8, name=f"w_plane{u}", align_bytes=64) for u in range(2)]
         dealt = [[sb.tile([P, 2, LH, PACK], BF16, name=f"dealt{u}_{h}", align_bytes=64) for h in range(2)] for u in range(2)]
 
-        def deal(copy, u, h):
-            cols = w_raw[h][:].rearrange("p j (l t) -> p l j t", t=PACK)[:, :, :, 2 * u : 2 * u + 2]
-            copy(out=dealt[u][h][:].rearrange("p e l j -> p l j e"), in_=cols)
+        def deal(copy, u, h, a, b):
+            cols = w_raw[h][:].rearrange("p j (l t) -> p l j t", t=PACK)[:, a:b, :, 2 * u : 2 * u + 2]
+            copy(out=dealt[u][h][:].rearrange("p e l j -> p l j e")[:, a:b], in_=cols)
 
         def quantize_w(u, h):
             for e in range(2):
@@ -78,11 +79,16 @@ def tile_picked_wkvput_tanh_lo_kernel(tc, x_words, x_scales, mem, w1, slot, out_
                     in_=dealt[u][h][:, e].rearrange("p l j -> p (l j)"),
                 )
 
-        for h in range(2):
-            deal(nc.vector.tensor_copy, 0, h)
-            deal(nc.scalar.copy, 1, h)
-            quantize_w(0, h)
-            quantize_w(1, h)
+        deal(nc.vector.tensor_copy, 0, 0, 0, LH)
+        deal(nc.scalar.copy, 1, 0, 0, LH)
+        quantize_w(0, 0)
+        quantize_w(1, 0)
+        deal(nc.vector.tensor_copy, 0, 1, 0, DEAL_FIRST)
+        deal(nc.scalar.copy, 0, 1, DEAL_FIRST, LH)
+        deal(nc.vector.tensor_copy, 1, 1, 0, LH // 2)
+        deal(nc.scalar.copy, 1, 1, LH // 2, LH)
+        quantize_w(0, 1)
+        quantize_w(1, 1)
 
         values = [sb.tile([P, T], F32, name=f"y{t}") for t in range(PACK)]
 

@@ -23,7 +23,7 @@ QUADS = 4
 HALF = N // 2
 LH = HALF // PACK
 TH = T // 2
-SHARED = 192
+SHARED = 224
 SPLIT = 576
 DEAL_FIRST = 40
 POOL_COLS = 384
@@ -126,17 +126,16 @@ def tile_picked_wkvput_tanh_lo_kernel(tc, x_words, x_scales, mem, w1, slot, out_
 
         for t in range(PACK):
             project(t, 0, TH)
-        project(0, TH, T)
-        project(1, TH, T)
+        for t in (1, 2, 0):
+            project(t, TH, T)
 
         vector_scatter(0, 0, TH)
-        vector_scatter(0, TH, T)
+        scalar_scatter(0, TH, T)
         store(0)
         gpsimd_round(pairs[:, 0, :, 0], window[0][:])
 
-        scalar_scatter(1, 0, TH)
-        project(2, TH, T)
         project(3, TH, T)
+        vector_scatter(1, 0, TH)
         scalar_scatter(1, TH, T)
         store(1)
         gpsimd_round(pairs[:, 0, :, 1], window[1][:])

@@ -23,10 +23,9 @@ QUADS = 4
 HALF = N // 2
 LH = HALF // PACK
 TH = T // 2
-SHARED = 224
+SHARED = 128
 SPLIT = 576
 DEAL_FIRST = 40
-POOL_COLS = 384
 
 
 def tile_picked_wkvput_tanh_lo_kernel(tc, x_words, x_scales, mem, w1, slot, out_0, out_1, out_2):
@@ -90,7 +89,8 @@ def tile_picked_wkvput_tanh_lo_kernel(tc, x_words, x_scales, mem, w1, slot, out_
         quantize_w(0, 1)
         quantize_w(1, 1)
 
-        values = [sb.tile([P, T], F32, name=f"y{t}") for t in range(PACK)]
+        pair_words = sb.tile([P, 2 * U], F32, name="pair_words")
+        values = [sb.tile([P, T], F32, name=f"y{t}")[:] for t in range(PACK - 1)] + [pair_words[:, U : U + T]]
 
         def project(t, a, b):
             cols = slice((t % 2) * P, (t % 2 + 1) * P)
@@ -115,18 +115,14 @@ def tile_picked_wkvput_tanh_lo_kernel(tc, x_words, x_scales, mem, w1, slot, out_
         def store(t):
             nc.sync.dma_start(out=rows_of(out_0, t), in_=window[t][:])
 
-        pair_words = sb.tile([P, 2 * U], F32, name="pair_words")
         pairs = pair_words[:].bitcast(BF16).rearrange("p (u c e) -> p u c e", u=2, e=2)
-
-        def twice(a, b):
-            return window[2][:, a:b].unsqueeze(2).to_broadcast([P, b - a, 2])
 
         def gpsimd_round(out, in_):
             nc.gpsimd.tensor_scalar(out=out, in0=in_, scalar1=1.0, scalar2=0.0, op0=MULT, op1=ADD)
 
         for t in range(PACK):
             project(t, 0, TH)
-        for t in (1, 2, 0):
+        for t in (1, 2, 0, 3):
             project(t, TH, T)
 
         vector_scatter(0, 0, TH)
@@ -134,7 +130,6 @@ def tile_picked_wkvput_tanh_lo_kernel(tc, x_words, x_scales, mem, w1, slot, out_
         store(0)
         gpsimd_round(pairs[:, 0, :, 0], window[0][:])
 
-        project(3, TH, T)
         vector_scatter(1, 0, TH)
         scalar_scatter(1, TH, T)
         store(1)
@@ -143,12 +138,11 @@ def tile_picked_wkvput_tanh_lo_kernel(tc, x_words, x_scales, mem, w1, slot, out_
         vector_scatter(2, 0, SHARED)
         scalar_scatter(2, SHARED, T)
         store(2)
-        gpsimd_round(pairs[:, 1, 0:POOL_COLS], twice(0, POOL_COLS))
-        nc.scalar.copy(out=pairs[:, 1, POOL_COLS:SPLIT], in_=twice(POOL_COLS, SPLIT))
         nc.scalar.copy(out=pairs[:, 1, SPLIT:U, 0], in_=window[2][:, SPLIT:U])
 
         vector_scatter(3, 0, T)
         store(3)
+        nc.vector.tensor_copy(out=pairs[:, 1, 0:SPLIT, 0], in_=window[2][:, 0:SPLIT])
         grouped = sb.tile([P, U, PACK], BF16, name="grouped", align_bytes=64)
         for cuts, copy, word in (((0, 256, SPLIT), nc.vector.tensor_copy, I32), ((SPLIT, 768, U), nc.scalar.copy, U32)):
             words = pair_words[:].bitcast(word).rearrange("p (u c) -> p c u", u=2)

@@ -24,6 +24,7 @@ HALF = N // 2
 LH = HALF // PACK
 TH = T // 2
 SHARED = 128
+FIRST = 192
 SPLIT = 576
 DEAL_FIRST = 40
 
@@ -122,16 +123,16 @@ def tile_picked_wkvput_tanh_lo_kernel(tc, x_words, x_scales, mem, w1, slot, out_
 
         for t in range(PACK):
             project(t, 0, TH)
-        for t in (1, 2, 0, 3):
+        for t in (1, 0, 2, 3):
             project(t, TH, T)
 
-        vector_scatter(0, 0, TH)
-        scalar_scatter(0, TH, T)
+        vector_scatter(0, 0, FIRST)
+        scalar_scatter(0, FIRST, T)
         store(0)
         gpsimd_round(pairs[:, 0, :, 0], window[0][:])
 
-        vector_scatter(1, 0, TH)
-        scalar_scatter(1, TH, T)
+        vector_scatter(1, 0, T - FIRST)
+        scalar_scatter(1, T - FIRST, T)
         store(1)
         gpsimd_round(pairs[:, 0, :, 1], window[1][:])
 

@@ -20,13 +20,11 @@ ADD = mybir.AluOpType.add
 P = 128
 PACK = 4
 QUADS = 4
-HALF = N // 2
-LH = HALF // PACK
 TH = T // 2
 SHARED = 128
 FIRST = 192
 SPLIT = 576
-DEAL_FIRST = 40
+DEAL_FIRST = 80
 
 
 def tile_picked_wkvput_tanh_lo_kernel(tc, x_words, x_scales, mem, w1, slot, out_0, out_1, out_2):
@@ -42,16 +40,16 @@ def tile_picked_wkvput_tanh_lo_kernel(tc, x_words, x_scales, mem, w1, slot, out_
         def rows_of(dram, t):
             return dram.rearrange("(p t) u -> p t u", t=PACK)[:, t, :]
 
-        w_rows = w1.rearrange("(p j) n -> p j n", j=PACK)
+        w_rows = w1.rearrange("(p j) n -> p (j n)", j=PACK)
         x_rows = x_words[0].rearrange("p n t -> p (n t)").bitcast(I32)
-        w_raw = [sb.tile([P, PACK, HALF], F32, name=f"w_raw{h}") for h in range(2)]
+        w_raw = [sb.tile([P, 2 * N], F32, name=f"w_raw{h}") for h in range(2)]
         window = [sb.tile([P, U], F32, name=f"window{t}") for t in range(PACK)]
 
         def load_scales(q):
             nc.sync.dma_start(out=x_plane[32 * q : 32 * q + 4, :].bitcast(I32), in_=x_scales[0, 4 * q : 4 * q + 4, :].bitcast(I32))
 
         for h in range(2):
-            nc.sync.dma_start(out=w_raw[h][:], in_=w_rows[:, :, h * HALF : (h + 1) * HALF])
+            nc.sync.dma_start(out=w_raw[h][:], in_=w_rows[:, 2 * N * h : 2 * N * (h + 1)])
             load_scales(h)
         for q in range(2, QUADS):
             load_scales(q)
@@ -64,31 +62,24 @@ def tile_picked_wkvput_tanh_lo_kernel(tc, x_words, x_scales, mem, w1, slot, out_
 
         w_codes = [sb.tile([P, 2 * P], U32, name=f"w_codes{u}", align_bytes=64) for u in range(2)]
         w_plane = [sb.tile([P, 2 * P], U8, name=f"w_plane{u}", align_bytes=64) for u in range(2)]
-        dealt = [[sb.tile([P, 2, LH, PACK], BF16, name=f"dealt{u}_{h}", align_bytes=64) for h in range(2)] for u in range(2)]
+        dealt = [sb.tile([P, 2, P, PACK], BF16, name=f"dealt{u}", align_bytes=64) for u in range(2)]
 
         def deal(copy, u, h, a, b):
-            cols = w_raw[h][:].rearrange("p j (l t) -> p l j t", t=PACK)[:, a:b, :, 2 * u : 2 * u + 2]
-            copy(out=dealt[u][h][:].rearrange("p e l j -> p l j e")[:, a:b], in_=cols)
+            cols = w_raw[h][:].rearrange("p (j l t) -> p l j t", j=2, t=PACK)[:, a:b, :, 2 * u : 2 * u + 2]
+            copy(out=dealt[u][:].rearrange("p e l j -> p l j e")[:, a:b, 2 * h : 2 * h + 2], in_=cols)
 
-        def quantize_w(u, h):
+        for h in range(2):
+            for u in range(2):
+                deal(nc.vector.tensor_copy, u, h, 0, DEAL_FIRST)
+                deal(nc.scalar.copy, u, h, DEAL_FIRST, P)
+        for u in range(2):
             for e in range(2):
-                cols = slice(e * P + h * LH, e * P + (h + 1) * LH)
+                cols = slice(e * P, (e + 1) * P)
                 nc.vector.quantize_mx(
                     out=w_codes[u][:, cols].bitcast(FP8X4),
                     scales=w_plane[u][:, cols],
-                    in_=dealt[u][h][:, e].rearrange("p l j -> p (l j)"),
+                    in_=dealt[u][:, e].rearrange("p l j -> p (l j)"),
                 )
-
-        deal(nc.vector.tensor_copy, 0, 0, 0, LH)
-        deal(nc.scalar.copy, 1, 0, 0, LH)
-        quantize_w(0, 0)
-        quantize_w(1, 0)
-        deal(nc.vector.tensor_copy, 0, 1, 0, DEAL_FIRST)
-        deal(nc.scalar.copy, 0, 1, DEAL_FIRST, LH)
-        deal(nc.vector.tensor_copy, 1, 1, 0, LH // 2)
-        deal(nc.scalar.copy, 1, 1, LH // 2, LH)
-        quantize_w(0, 1)
-        quantize_w(1, 1)
 
         pair_words = sb.tile([P, 2 * U], F32, name="pair_words")
         values = [sb.tile([P, T], F32, name=f"y{t}")[:] for t in range(PACK - 1)] + [pair_words[:, U : U + T]]

@@ -25,6 +25,7 @@ SHARED = 128
 FIRST = 192
 SPLIT = 576
 DEAL_FIRST = 80
+DEAL_LAST = 48
 
 
 def tile_picked_wkvput_tanh_lo_kernel(tc, x_words, x_scales, mem, w1, slot, out_0, out_1, out_2):
@@ -64,22 +65,31 @@ def tile_picked_wkvput_tanh_lo_kernel(tc, x_words, x_scales, mem, w1, slot, out_
         w_plane = [sb.tile([P, 2 * P], U8, name=f"w_plane{u}", align_bytes=64) for u in range(2)]
         dealt = [sb.tile([P, 2, P, PACK], BF16, name=f"dealt{u}", align_bytes=64) for u in range(2)]
 
-        def deal(copy, u, h, a, b):
-            cols = w_raw[h][:].rearrange("p (j l t) -> p l j t", j=2, t=PACK)[:, a:b, :, 2 * u : 2 * u + 2]
-            copy(out=dealt[u][:].rearrange("p e l j -> p l j e")[:, a:b, 2 * h : 2 * h + 2], in_=cols)
+        def deal(copy, h, planes, a, b):
+            u, e = divmod(planes.start, 2)
+            cols = w_raw[h][:].rearrange("p (j l t) -> p l j t", j=2, t=PACK)[:, a:b, :, planes]
+            copy(out=dealt[u][:].rearrange("p e l j -> p l j e")[:, a:b, 2 * h : 2 * h + 2, e : e + planes.stop - planes.start], in_=cols)
 
-        for h in range(2):
-            for u in range(2):
-                deal(nc.vector.tensor_copy, u, h, 0, DEAL_FIRST)
-                deal(nc.scalar.copy, u, h, DEAL_FIRST, P)
+        def quantize_w(t):
+            cols = slice((t % 2) * P, (t % 2 + 1) * P)
+            nc.vector.quantize_mx(
+                out=w_codes[t // 2][:, cols].bitcast(FP8X4),
+                scales=w_plane[t // 2][:, cols],
+                in_=dealt[t // 2][:, t % 2].rearrange("p l j -> p (l j)"),
+            )
+
         for u in range(2):
-            for e in range(2):
-                cols = slice(e * P, (e + 1) * P)
-                nc.vector.quantize_mx(
-                    out=w_codes[u][:, cols].bitcast(FP8X4),
-                    scales=w_plane[u][:, cols],
-                    in_=dealt[u][:, e].rearrange("p l j -> p (l j)"),
-                )
+            deal(nc.vector.tensor_copy, 0, slice(2 * u, 2 * u + 2), 0, DEAL_FIRST)
+            deal(nc.scalar.copy, 0, slice(2 * u, 2 * u + 2), DEAL_FIRST, P)
+        for t in range(2):
+            deal(nc.vector.tensor_copy, 1, slice(t, t + 1), 0, DEAL_FIRST)
+            deal(nc.scalar.copy, 1, slice(t, t + 1), DEAL_FIRST, P)
+        for t in range(2, PACK):
+            deal(nc.scalar.copy, 1, slice(t, t + 1), DEAL_LAST, P)
+        quantize_w(0)
+        deal(nc.vector.tensor_copy, 1, slice(2, 4), 0, DEAL_LAST)
+        for t in range(1, PACK):
+            quantize_w(t)
 
         pair_words = sb.tile([P, 2 * U], F32, name="pair_words")
         values = [sb.tile([P, T], F32, name=f"y{t}")[:] for t in range(PACK - 1)] + [pair_words[:, U : U + T]]

@@ -23,6 +23,7 @@ QUADS = 4
 TH = T // 2
 SHARED = 128
 FIRST = 192
+OWN = 960
 SPLIT = 576
 DEAL_FIRST = 80
 DEAL_LAST = 48
@@ -91,8 +92,9 @@ def tile_picked_wkvput_tanh_lo_kernel(tc, x_words, x_scales, mem, w1, slot, out_
         for t in range(1, PACK):
             quantize_w(t)
 
-        pair_words = sb.tile([P, 2 * U], F32, name="pair_words")
-        values = [sb.tile([P, T], F32, name=f"y{t}")[:] for t in range(PACK - 1)] + [pair_words[:, U : U + T]]
+        pitch = OWN + T
+        pair_words = sb.tile([P, 2 * pitch], F32, name="pair_words")
+        values = [sb.tile([P, T], F32, name=f"y{t}")[:] for t in range(2)] + [pair_words[:, OWN:pitch], pair_words[:, pitch : pitch + T]]
 
         def project(t, a, b):
             cols = slice((t % 2) * P, (t % 2 + 1) * P)
@@ -130,16 +132,18 @@ def tile_picked_wkvput_tanh_lo_kernel(tc, x_words, x_scales, mem, w1, slot, out_
         vector_scatter(0, 0, FIRST)
         scalar_scatter(0, FIRST, T)
         store(0)
-        gpsimd_round(pairs[:, 0, :, 0], window[0][:])
+        gpsimd_round(pairs[:, 0, 0:OWN, 0], window[0][:, 0:OWN])
 
         vector_scatter(1, 0, T - FIRST)
         scalar_scatter(1, T - FIRST, T)
         store(1)
-        gpsimd_round(pairs[:, 0, :, 1], window[1][:])
+        gpsimd_round(pairs[:, 0, 0:OWN, 1], window[1][:, 0:OWN])
 
         vector_scatter(2, 0, SHARED)
         scalar_scatter(2, SHARED, T)
         store(2)
+        for e in range(2):
+            nc.scalar.copy(out=pairs[:, 0, OWN:U, e], in_=window[e][:, OWN:U])
         nc.scalar.copy(out=pairs[:, 1, SPLIT:U, 0], in_=window[2][:, SPLIT:U])
 
         vector_scatter(3, 0, T)

@@ -23,8 +23,9 @@ QUADS = 4
 TH = T // 2
 SHARED = 128
 FIRST = 192
+SECOND = 288
 OWN = 960
-SPLIT = 576
+SPLIT = 608
 DEAL_FIRST = 80
 DEAL_LAST = 48
 
@@ -94,7 +95,7 @@ def tile_picked_wkvput_tanh_lo_kernel(tc, x_words, x_scales, mem, w1, slot, out_
 
         pitch = OWN + T
         pair_words = sb.tile([P, 2 * pitch], F32, name="pair_words")
-        values = [sb.tile([P, T], F32, name=f"y{t}")[:] for t in range(2)] + [pair_words[:, OWN:pitch], pair_words[:, pitch : pitch + T]]
+        values = [sb.tile([P, T], F32, name=f"y{t}")[:] for t in range(2)] + [pair_words[:, OWN:pitch], pair_words[:, pitch + 288 : pitch + 288 + T]]
 
         def project(t, a, b):
             cols = slice((t % 2) * P, (t % 2 + 1) * P)
@@ -134,8 +135,8 @@ def tile_picked_wkvput_tanh_lo_kernel(tc, x_words, x_scales, mem, w1, slot, out_
         store(0)
         gpsimd_round(pairs[:, 0, 0:OWN, 0], window[0][:, 0:OWN])
 
-        vector_scatter(1, 0, T - FIRST)
-        scalar_scatter(1, T - FIRST, T)
+        vector_scatter(1, 0, SECOND)
+        scalar_scatter(1, SECOND, T)
         store(1)
         gpsimd_round(pairs[:, 0, 0:OWN, 1], window[1][:, 0:OWN])
 
@@ -144,16 +145,15 @@ def tile_picked_wkvput_tanh_lo_kernel(tc, x_words, x_scales, mem, w1, slot, out_
         store(2)
         for e in range(2):
             nc.scalar.copy(out=pairs[:, 0, OWN:U, e], in_=window[e][:, OWN:U])
-        nc.scalar.copy(out=pairs[:, 1, SPLIT:U, 0], in_=window[2][:, SPLIT:U])
 
         vector_scatter(3, 0, T)
         store(3)
-        nc.vector.tensor_copy(out=pairs[:, 1, 0:SPLIT, 0], in_=window[2][:, 0:SPLIT])
         grouped = sb.tile([P, U, PACK], BF16, name="grouped", align_bytes=64)
-        for cuts, copy, word in (((0, 256, SPLIT), nc.vector.tensor_copy, I32), ((SPLIT, 768, U), nc.scalar.copy, U32)):
+        for cuts, copy, word in (((0, 320, SPLIT), nc.vector.tensor_copy, I32), ((SPLIT, 768, U), nc.scalar.copy, U32)):
             words = pair_words[:].bitcast(word).rearrange("p (u c) -> p c u", u=2)
+            copy(out=pairs[:, 1, cuts[0] : cuts[-1], 1], in_=window[3][:, cuts[0] : cuts[-1]])
             for a, b in zip(cuts, cuts[1:]):
-                copy(out=pairs[:, 1, a:b, 1], in_=window[3][:, a:b])
+                copy(out=pairs[:, 1, a:b, 0], in_=window[2][:, a:b])
             for a, b in zip(cuts, cuts[1:]):
                 copy(out=grouped[:, a:b, :].bitcast(word), in_=words[:, a:b, :])
 

@@ -21,11 +21,11 @@ P = 128
 PACK = 4
 QUADS = 4
 TH = T // 2
-SHARED = 128
+SHARED = 160
 FIRST = 192
-SECOND = 288
-OWN = 960
-SPLIT = 608
+SECOND = 320
+EARLY = 960
+SPLIT = 560
 DEAL_FIRST = 80
 DEAL_LAST = 48
 
@@ -56,12 +56,13 @@ def tile_picked_wkvput_tanh_lo_kernel(tc, x_words, x_scales, mem, w1, slot, out_
             load_scales(h)
         for q in range(2, QUADS):
             load_scales(q)
-        nc.sync.dma_start(out=x_codes[:, 0:TH].bitcast(I32), in_=x_rows[:, 0:TH])
+        nc.sync.dma_start(out=x_codes[:].bitcast(I32), in_=x_rows)
         nc.sync.dma_start(out=window[0][:], in_=rows_of(mem, 0))
         nc.sync.dma_start(offsets[:], slot)
-        nc.sync.dma_start(out=x_codes[:, TH:T].bitcast(I32), in_=x_rows[:, TH:T])
-        for t in range(1, PACK):
-            nc.sync.dma_start(out=window[t][:], in_=rows_of(mem, t))
+        nc.sync.dma_start(out=window[1][:], in_=rows_of(mem, 1))
+        nc.sync.dma_start(out=window[3][:, 0:EARLY], in_=rows_of(mem, 3)[:, 0:EARLY])
+        nc.sync.dma_start(out=window[2][:], in_=rows_of(mem, 2))
+        nc.sync.dma_start(out=window[3][:, EARLY:U], in_=rows_of(mem, 3)[:, EARLY:U])
 
         w_codes = [sb.tile([P, 2 * P], U32, name=f"w_codes{u}", align_bytes=64) for u in range(2)]
         w_plane = [sb.tile([P, 2 * P], U8, name=f"w_plane{u}", align_bytes=64) for u in range(2)]
@@ -93,9 +94,8 @@ def tile_picked_wkvput_tanh_lo_kernel(tc, x_words, x_scales, mem, w1, slot, out_
         for t in range(1, PACK):
             quantize_w(t)
 
-        pitch = OWN + T
-        pair_words = sb.tile([P, 2 * pitch], F32, name="pair_words")
-        values = [sb.tile([P, T], F32, name=f"y{t}")[:] for t in range(2)] + [pair_words[:, OWN:pitch], pair_words[:, pitch + 288 : pitch + 288 + T]]
+        pair_words = sb.tile([P, 2 * U], F32, name="pair_words")
+        values = [sb.tile([P, T], F32, name=f"y{t}")[:] for t in range(PACK)]
 
         def project(t, a, b):
             cols = slice((t % 2) * P, (t % 2 + 1) * P)
@@ -133,33 +133,31 @@ def tile_picked_wkvput_tanh_lo_kernel(tc, x_words, x_scales, mem, w1, slot, out_
         vector_scatter(0, 0, FIRST)
         scalar_scatter(0, FIRST, T)
         store(0)
-        gpsimd_round(pairs[:, 0, 0:OWN, 0], window[0][:, 0:OWN])
+        gpsimd_round(pairs[:, 0, :, 0], window[0][:])
 
         vector_scatter(1, 0, SECOND)
         scalar_scatter(1, SECOND, T)
         store(1)
-        gpsimd_round(pairs[:, 0, 0:OWN, 1], window[1][:, 0:OWN])
+        gpsimd_round(pairs[:, 0, :, 1], window[1][:])
 
         vector_scatter(2, 0, SHARED)
         scalar_scatter(2, SHARED, T)
         store(2)
-        for e in range(2):
-            nc.scalar.copy(out=pairs[:, 0, OWN:U, e], in_=window[e][:, OWN:U])
 
         vector_scatter(3, 0, T)
         store(3)
         grouped = sb.tile([P, U, PACK], BF16, name="grouped", align_bytes=64)
         for cuts, copy, word in (((0, 320, SPLIT), nc.vector.tensor_copy, I32), ((SPLIT, 768, U), nc.scalar.copy, U32)):
             words = pair_words[:].bitcast(word).rearrange("p (u c) -> p c u", u=2)
-            copy(out=pairs[:, 1, cuts[0] : cuts[-1], 1], in_=window[3][:, cuts[0] : cuts[-1]])
+            copy(out=pairs[:, 1, cuts[0] : cuts[-1], 0], in_=window[2][:, cuts[0] : cuts[-1]])
             for a, b in zip(cuts, cuts[1:]):
-                copy(out=pairs[:, 1, a:b, 0], in_=window[2][:, a:b])
+                copy(out=pairs[:, 1, a:b, 1], in_=window[3][:, a:b])
             for a, b in zip(cuts, cuts[1:]):
                 copy(out=grouped[:, a:b, :].bitcast(word), in_=words[:, a:b, :])
 
         o_plane = sb.tile([P, U], U8, name="o_plane", align_bytes=64)
         words_out = out_1[0].rearrange("p n t -> p (n t)").bitcast(I32)
-        for cuts in [(0, 256, 512), (512, 768), (768, 1024)]:
+        for cuts in [(0, 256, 384), (384, 640, 768), (768, 1024)]:
             codes = sb.tile([P, cuts[-1] - cuts[0]], U32, name=f"o_codes{cuts[0]}", align_bytes=64)
             for a, b in zip(cuts, cuts[1:]):
                 nc.vector.quantize_mx(

@@ -24,6 +24,7 @@ TH = T // 2
 SHARED = 160
 FIRST = 192
 SECOND = 320
+OWN = 928
 EARLY = 960
 SPLIT = 560
 DEAL_FIRST = 80
@@ -94,8 +95,9 @@ def tile_picked_wkvput_tanh_lo_kernel(tc, x_words, x_scales, mem, w1, slot, out_
         for t in range(1, PACK):
             quantize_w(t)
 
-        pair_words = sb.tile([P, 2 * U], F32, name="pair_words")
-        values = [sb.tile([P, T], F32, name=f"y{t}")[:] for t in range(PACK)]
+        pitch = OWN + T
+        pair_words = sb.tile([P, 2 * pitch], F32, name="pair_words")
+        values = [pair_words[:, OWN:pitch] if t == 2 else sb.tile([P, T], F32, name=f"y{t}")[:] for t in range(PACK)]
 
         def project(t, a, b):
             cols = slice((t % 2) * P, (t % 2 + 1) * P)
@@ -133,16 +135,18 @@ def tile_picked_wkvput_tanh_lo_kernel(tc, x_words, x_scales, mem, w1, slot, out_
         vector_scatter(0, 0, FIRST)
         scalar_scatter(0, FIRST, T)
         store(0)
-        gpsimd_round(pairs[:, 0, :, 0], window[0][:])
+        gpsimd_round(pairs[:, 0, 0:OWN, 0], window[0][:, 0:OWN])
 
         vector_scatter(1, 0, SECOND)
         scalar_scatter(1, SECOND, T)
         store(1)
-        gpsimd_round(pairs[:, 0, :, 1], window[1][:])
+        gpsimd_round(pairs[:, 0, 0:OWN, 1], window[1][:, 0:OWN])
 
         vector_scatter(2, 0, SHARED)
         scalar_scatter(2, SHARED, T)
         store(2)
+        for e in range(2):
+            nc.scalar.copy(out=pairs[:, 0, OWN:U, e], in_=window[e][:, OWN:U])
 
         vector_scatter(3, 0, T)
         store(3)

@@ -25,7 +25,7 @@ SHARED = 160
 FIRST = 192
 SECOND = 320
 OWN = 928
-EARLY = 960
+EARLY = 768
 SPLIT = 560
 DEAL_FIRST = 80
 DEAL_LAST = 48
@@ -54,8 +54,7 @@ def tile_picked_wkvput_tanh_lo_kernel(tc, x_words, x_scales, mem, w1, slot, out_
 
         for h in range(2):
             nc.sync.dma_start(out=w_raw[h][:], in_=w_rows[:, 2 * N * h : 2 * N * (h + 1)])
-            load_scales(h)
-        for q in range(2, QUADS):
+        for q in range(QUADS):
             load_scales(q)
         nc.sync.dma_start(out=x_codes[:].bitcast(I32), in_=x_rows)
         nc.sync.dma_start(out=window[0][:], in_=rows_of(mem, 0))

@@ -26,7 +26,7 @@ FIRST = 192
 SECOND = 320
 OWN = 928
 EARLY = 768
-SPLIT = 560
+SPLIT = 528
 DEAL_FIRST = 80
 DEAL_LAST = 48
 
@@ -98,9 +98,12 @@ def tile_picked_wkvput_tanh_lo_kernel(tc, x_words, x_scales, mem, w1, slot, out_
         pair_words = sb.tile([P, 2 * pitch], F32, name="pair_words")
         values = [pair_words[:, OWN:pitch] if t == 2 else sb.tile([P, T], F32, name=f"y{t}")[:] for t in range(PACK)]
 
+        made = []
+
         def project(t, a, b):
             cols = slice((t % 2) * P, (t % 2 + 1) * P)
-            acc = ps.tile([P, b - a], F32, name=f"acc{t}_{a}")
+            acc = ps.tile([P, b - a], F32, name=f"acc{t}_{a}", tag=f"bank{len(made) % 8}")
+            made.append((t, a))
             nc.tensor.matmul_mx(
                 out=acc[:],
                 lhsT=w_codes[t // 2][:, cols].bitcast(FP8X4),
@@ -126,10 +129,10 @@ def tile_picked_wkvput_tanh_lo_kernel(tc, x_words, x_scales, mem, w1, slot, out_
         def gpsimd_round(out, in_):
             nc.gpsimd.tensor_scalar(out=out, in0=in_, scalar1=1.0, scalar2=0.0, op0=MULT, op1=ADD)
 
-        for t in range(PACK):
-            project(t, 0, TH)
-        for t in (1, 0, 2, 3):
-            project(t, TH, T)
+        project(0, 0, P)
+        project(0, P, TH)
+        for t, a in ((1, 0), (1, TH), (2, 0), (3, 0), (0, TH), (2, TH), (3, TH)):
+            project(t, a, a + TH)
 
         vector_scatter(0, 0, FIRST)
         scalar_scatter(0, FIRST, T)
@@ -150,7 +153,7 @@ def tile_picked_wkvput_tanh_lo_kernel(tc, x_words, x_scales, mem, w1, slot, out_
         vector_scatter(3, 0, T)
         store(3)
         grouped = sb.tile([P, U, PACK], BF16, name="grouped", align_bytes=64)
-        for cuts, copy, word in (((0, 320, SPLIT), nc.vector.tensor_copy, I32), ((SPLIT, 768, U), nc.scalar.copy, U32)):
+        for cuts, copy, word in (((0, 288, SPLIT), nc.vector.tensor_copy, I32), ((SPLIT, 768, U), nc.scalar.copy, U32)):
             words = pair_words[:].bitcast(word).rearrange("p (u c) -> p c u", u=2)
             copy(out=pairs[:, 1, cuts[0] : cuts[-1], 0], in_=window[2][:, cuts[0] : cuts[-1]])
             for a, b in zip(cuts, cuts[1:]):

@@ -26,7 +26,7 @@ FIRST = 192
 SECOND = 320
 OWN = 928
 EARLY = 768
-SPLIT = 528
+SPLIT = 592
 DEAL_FIRST = 80
 DEAL_LAST = 48
 
@@ -153,7 +153,7 @@ def tile_picked_wkvput_tanh_lo_kernel(tc, x_words, x_scales, mem, w1, slot, out_
         vector_scatter(3, 0, T)
         store(3)
         grouped = sb.tile([P, U, PACK], BF16, name="grouped", align_bytes=64)
-        for cuts, copy, word in (((0, 288, SPLIT), nc.vector.tensor_copy, I32), ((SPLIT, 768, U), nc.scalar.copy, U32)):
+        for cuts, copy, word in (((0, 320, SPLIT), nc.vector.tensor_copy, I32), ((SPLIT, 768, U), nc.scalar.copy, U32)):
             words = pair_words[:].bitcast(word).rearrange("p (u c) -> p c u", u=2)
             copy(out=pairs[:, 1, cuts[0] : cuts[-1], 0], in_=window[2][:, cuts[0] : cuts[-1]])
             for a, b in zip(cuts, cuts[1:]):

@@ -24,7 +24,7 @@ TH = T // 2
 SHARED = 160
 FIRST = 192
 SECOND = 320
-OWN = 928
+OWN = 896
 EARLY = 768
 SPLIT = 592
 DEAL_FIRST = 80

@@ -173,5 +173,5 @@ def tile_picked_wkvput_tanh_lo_kernel(tc, x_words, x_scales, mem, w1, slot, out_
                 )
             nc.sync.dma_start(out=words_out[:, cuts[0] : cuts[-1]], in_=codes[:].bitcast(I32))
         for q in range(QUADS):
-            queue = nc.scalar if q % 2 == 0 else nc.sync
+            queue = nc.sync if q == QUADS - 1 else nc.scalar
             queue.dma_start(out=out_2[0, 4 * q : 4 * q + 4, :].bitcast(I32), in_=o_plane[32 * q : 32 * q + 4, :].bitcast(I32))

@@ -173,5 +173,4 @@ def tile_picked_wkvput_tanh_lo_kernel(tc, x_words, x_scales, mem, w1, slot, out_
                 )
             nc.sync.dma_start(out=words_out[:, cuts[0] : cuts[-1]], in_=codes[:].bitcast(I32))
         for q in range(QUADS):
-            queue = nc.sync if q == QUADS - 1 else nc.scalar
-            queue.dma_start(out=out_2[0, 4 * q : 4 * q + 4, :].bitcast(I32), in_=o_plane[32 * q : 32 * q + 4, :].bitcast(I32))
+            nc.scalar.dma_start(out=out_2[0, 4 * q : 4 * q + 4, :].bitcast(I32), in_=o_plane[32 * q : 32 * q + 4, :].bitcast(I32))

@@ -21,12 +21,12 @@ P = 128
 PACK = 4
 QUADS = 4
 TH = T // 2
-SHARED = 160
+SHARED = 192
 FIRST = 192
 SECOND = 320
 OWN = 896
 EARLY = 768
-SPLIT = 592
+SPLIT = 512
 DEAL_FIRST = 80
 DEAL_LAST = 48
 
@@ -153,7 +153,7 @@ def tile_picked_wkvput_tanh_lo_kernel(tc, x_words, x_scales, mem, w1, slot, out_
         vector_scatter(3, 0, T)
         store(3)
         grouped = sb.tile([P, U, PACK], BF16, name="grouped", align_bytes=64)
-        for cuts, copy, word in (((0, 320, SPLIT), nc.vector.tensor_copy, I32), ((SPLIT, 768, U), nc.scalar.copy, U32)):
+        for cuts, copy, word in (((0, 256, SPLIT), nc.vector.tensor_copy, I32), ((SPLIT, 768, 896, U), nc.scalar.copy, U32)):
             words = pair_words[:].bitcast(word).rearrange("p (u c) -> p c u", u=2)
             copy(out=pairs[:, 1, cuts[0] : cuts[-1], 0], in_=window[2][:, cuts[0] : cuts[-1]])
             for a, b in zip(cuts, cuts[1:]):
@@ -163,7 +163,7 @@ def tile_picked_wkvput_tanh_lo_kernel(tc, x_words, x_scales, mem, w1, slot, out_
 
         o_plane = sb.tile([P, U], U8, name="o_plane", align_bytes=64)
         words_out = out_1[0].rearrange("p n t -> p (n t)").bitcast(I32)
-        for cuts in [(0, 256, 384), (384, 640, 768), (768, 1024)]:
+        for cuts in [(0, 256, 384), (384, 512, 768), (768, 896, 1024)]:
             codes = sb.tile([P, cuts[-1] - cuts[0]], U32, name=f"o_codes{cuts[0]}", align_bytes=64)
             for a, b in zip(cuts, cuts[1:]):
                 nc.vector.quantize_mx(
@@ -172,5 +172,5 @@ def tile_picked_wkvput_tanh_lo_kernel(tc, x_words, x_scales, mem, w1, slot, out_
                     in_=grouped[:, a:b, :].rearrange("p c t -> p (c t)"),
                 )
             nc.sync.dma_start(out=words_out[:, cuts[0] : cuts[-1]], in_=codes[:].bitcast(I32))
-        for q in range(QUADS):
-            nc.scalar.dma_start(out=out_2[0, 4 * q : 4 * q + 4, :].bitcast(I32), in_=o_plane[32 * q : 32 * q + 4, :].bitcast(I32))
+        for r in range(4):
+            nc.scalar.dma_start(out=out_2[0, r:16:4, :].bitcast(I32), in_=o_plane[r:P:32, :].bitcast(I32))

from contextlib import ExitStack

import concourse.mybir as mybir

K, T, N, U = 512, 512, 512, 1024
FLOPS = 2 * K * T * N

F32 = mybir.dt.float32
BF16 = mybir.dt.bfloat16
I32 = mybir.dt.int32
U32 = mybir.dt.uint32
U16 = mybir.dt.uint16
U8 = mybir.dt.uint8
FP8X4 = mybir.dt.float8_e4m3fn_x4
TANH = mybir.ActivationFunctionType.Tanh
COPY = mybir.ActivationFunctionType.Copy
MULT = mybir.AluOpType.mult
ADD = mybir.AluOpType.add

P = 128
PACK = 4
QUADS = 4
TH = T // 2
SHARED = 192
FIRST = 192
SECOND = 320
OWN = 896
EARLY = 768
SPLIT = 512
DEAL_FIRST = 80
DEAL_LAST = 48


def tile_picked_wkvput_tanh_lo_kernel(tc, x_words, x_scales, mem, w1, slot, out_0, out_1, out_2):
    nc = tc.nc
    with ExitStack() as ctx:
        sb = ctx.enter_context(tc.tile_pool(name="sb", bufs=1))
        ps = ctx.enter_context(tc.psum_pool(name="ps", bufs=1))

        offsets = sb.tile([P, T // 16], U16, name="offsets")
        x_codes = sb.tile([P, T], U32, name="x_codes", align_bytes=64)
        x_plane = sb.tile([P, T], U8, name="x_plane", align_bytes=64)

        def rows_of(dram, t):
            return dram.rearrange("(p t) u -> p t u", t=PACK)[:, t, :]

        w_rows = w1.rearrange("(p j) n -> p (j n)", j=PACK)
        x_rows = x_words[0].rearrange("p n t -> p (n t)").bitcast(I32)
        w_raw = [sb.tile([P, 2 * N], F32, name=f"w_raw{h}") for h in range(2)]
        window = [sb.tile([P, U], F32, name=f"window{t}") for t in range(PACK)]

        def load_scales(q):
            nc.sync.dma_start(out=x_plane[32 * q : 32 * q + 4, :].bitcast(I32), in_=x_scales[0, 4 * q : 4 * q + 4, :].bitcast(I32))

        for h in range(2):
            nc.sync.dma_start(out=w_raw[h][:], in_=w_rows[:, 2 * N * h : 2 * N * (h + 1)])
        for q in range(QUADS):
            load_scales(q)
        nc.sync.dma_start(out=x_codes[:].bitcast(I32), in_=x_rows)
        nc.sync.dma_start(out=window[0][:], in_=rows_of(mem, 0))
        nc.sync.dma_start(offsets[:], slot)
        nc.sync.dma_start(out=window[1][:], in_=rows_of(mem, 1))
        nc.sync.dma_start(out=window[3][:, 0:EARLY], in_=rows_of(mem, 3)[:, 0:EARLY])
        nc.sync.dma_start(out=window[2][:], in_=rows_of(mem, 2))
        nc.sync.dma_start(out=window[3][:, EARLY:U], in_=rows_of(mem, 3)[:, EARLY:U])

        w_codes = [sb.tile([P, 2 * P], U32, name=f"w_codes{u}", align_bytes=64) for u in range(2)]
        w_plane = [sb.tile([P, 2 * P], U8, name=f"w_plane{u}", align_bytes=64) for u in range(2)]
        dealt = [sb.tile([P, 2, P, PACK], BF16, name=f"dealt{u}", align_bytes=64) for u in range(2)]

        def deal(copy, h, planes, a, b):
            u, e = divmod(planes.start, 2)
            cols = w_raw[h][:].rearrange("p (j l t) -> p l j t", j=2, t=PACK)[:, a:b, :, planes]
            copy(out=dealt[u][:].rearrange("p e l j -> p l j e")[:, a:b, 2 * h : 2 * h + 2, e : e + planes.stop - planes.start], in_=cols)

        def quantize_w(t):
            cols = slice((t % 2) * P, (t % 2 + 1) * P)
            nc.vector.quantize_mx(
                out=w_codes[t // 2][:, cols].bitcast(FP8X4),
                scales=w_plane[t // 2][:, cols],
                in_=dealt[t // 2][:, t % 2].rearrange("p l j -> p (l j)"),
            )

        for u in range(2):
            deal(nc.vector.tensor_copy, 0, slice(2 * u, 2 * u + 2), 0, DEAL_FIRST)
            deal(nc.scalar.copy, 0, slice(2 * u, 2 * u + 2), DEAL_FIRST, P)
        for t in range(2):
            deal(nc.vector.tensor_copy, 1, slice(t, t + 1), 0, DEAL_FIRST)
            deal(nc.scalar.copy, 1, slice(t, t + 1), DEAL_FIRST, P)
        for t in range(2, PACK):
            deal(nc.scalar.copy, 1, slice(t, t + 1), DEAL_LAST, P)
        quantize_w(0)
        deal(nc.vector.tensor_copy, 1, slice(2, 4), 0, DEAL_LAST)
        for t in range(1, PACK):
            quantize_w(t)

        pitch = OWN + T
        pair_words = sb.tile([P, 2 * pitch], F32, name="pair_words")
        values = [pair_words[:, OWN:pitch] if t == 2 else sb.tile([P, T], F32, name=f"y{t}")[:] for t in range(PACK)]

        made = []

        def project(t, a, b):
            cols = slice((t % 2) * P, (t % 2 + 1) * P)
            acc = ps.tile([P, b - a], F32, name=f"acc{t}_{a}", tag=f"bank{len(made) % 8}")
            made.append((t, a))
            nc.tensor.matmul_mx(
                out=acc[:],
                lhsT=w_codes[t // 2][:, cols].bitcast(FP8X4),
                lhsT_scale=w_plane[t // 2][:, cols],
                rhs=x_codes[:, a:b].bitcast(FP8X4),
                rhs_scale=x_plane[:, a:b],
                start=True,
                stop=True,
            )
            nc.scalar.activation(values[t][:, a:b], acc[:], TANH)

        def vector_scatter(t, a, b):
            nc.vector.tensor_copy(window[t][:].indirect(offsets[:, a // 16 : b // 16]), values[t][:, a:b])

        def scalar_scatter(t, a, b):
            nc.scalar.activation(window[t][:].indirect(offsets[:, a // 16 : b // 16]), values[t][:, a:b], COPY)

        def store(t):
            nc.sync.dma_start(out=rows_of(out_0, t), in_=window[t][:])

        pairs = pair_words[:].bitcast(BF16).rearrange("p (u c e) -> p u c e", u=2, e=2)

        def gpsimd_round(out, in_):
            nc.gpsimd.tensor_scalar(out=out, in0=in_, scalar1=1.0, scalar2=0.0, op0=MULT, op1=ADD)

        project(0, 0, P)
        project(0, P, TH)
        for t, a in ((1, 0), (1, TH), (2, 0), (3, 0), (0, TH), (2, TH), (3, TH)):
            project(t, a, a + TH)

        vector_scatter(0, 0, FIRST)
        scalar_scatter(0, FIRST, T)
        store(0)
        gpsimd_round(pairs[:, 0, 0:OWN, 0], window[0][:, 0:OWN])

        vector_scatter(1, 0, SECOND)
        scalar_scatter(1, SECOND, T)
        store(1)
        gpsimd_round(pairs[:, 0, 0:OWN, 1], window[1][:, 0:OWN])

        vector_scatter(2, 0, SHARED)
        scalar_scatter(2, SHARED, T)
        store(2)
        for e in range(2):
            nc.scalar.copy(out=pairs[:, 0, OWN:U, e], in_=window[e][:, OWN:U])

        vector_scatter(3, 0, T)
        store(3)
        grouped = sb.tile([P, U, PACK], BF16, name="grouped", align_bytes=64)
        for cuts, copy, word in (((0, 256, SPLIT), nc.vector.tensor_copy, I32), ((SPLIT, 768, 896, U), nc.scalar.copy, U32)):
            words = pair_words[:].bitcast(word).rearrange("p (u c) -> p c u", u=2)
            copy(out=pairs[:, 1, cuts[0] : cuts[-1], 0], in_=window[2][:, cuts[0] : cuts[-1]])
            for a, b in zip(cuts, cuts[1:]):
                copy(out=pairs[:, 1, a:b, 1], in_=window[3][:, a:b])
            for a, b in zip(cuts, cuts[1:]):
                copy(out=grouped[:, a:b, :].bitcast(word), in_=words[:, a:b, :])

        o_plane = sb.tile([P, U], U8, name="o_plane", align_bytes=64)
        words_out = out_1[0].rearrange("p n t -> p (n t)").bitcast(I32)
        for cuts in [(0, 256, 384), (384, 512, 768), (768, 896, 1024)]:
            codes = sb.tile([P, cuts[-1] - cuts[0]], U32, name=f"o_codes{cuts[0]}", align_bytes=64)
            for a, b in zip(cuts, cuts[1:]):
                nc.vector.quantize_mx(
                    out=codes[:, a - cuts[0] : b - cuts[0]].bitcast(FP8X4),
                    scales=o_plane[:, a:b],
                    in_=grouped[:, a:b, :].rearrange("p c t -> p (c t)"),
                )
            nc.sync.dma_start(out=words_out[:, cuts[0] : cuts[-1]], in_=codes[:].bitcast(I32))
        for r in range(4):
            nc.scalar.dma_start(out=out_2[0, r:16:4, :].bitcast(I32), in_=o_plane[r:P:32, :].bitcast(I32))
